import numpy as np
import ml_dtypes


def mxq(x, axis, fmt="e4m3"):
    dtype, down = {"e4m3": (ml_dtypes.float8_e4m3fn, 7), "e5m2": (ml_dtypes.float8_e5m2, 14)}[fmt]
    v = np.moveaxis(np.asarray(x, np.float32).astype(ml_dtypes.bfloat16).astype(np.float64), axis, -1)
    blocks = v.reshape(v.shape[:-1] + (-1, 32))
    amax = np.abs(blocks).max(-1, keepdims=True)
    byte = np.maximum(np.where(amax > 0, np.frexp(amax)[1] - 1 + 127, 0) - down, 1)
    scale = np.exp2(byte - 127.0)
    codes = (blocks / scale).astype(np.float32).astype(dtype).astype(np.float64)
    return np.moveaxis((codes * scale).reshape(v.shape), -1, axis)


WIDE = False


def mx_kscale(k):
    if not WIDE:
        return np.ones(k)
    levels = np.array([10, -10, 5, -5, 0])
    if k % 512:
        return np.exp2(np.random.permutation(np.resize(levels, k // 32))).repeat(32)
    a = np.empty((k // 512, 16))
    for p in range(k // 512):
        a[p, :8] = np.random.permutation(np.resize(levels, 8))
        for g in range(8):
            far = levels[np.abs(levels - a[p, g]) >= 10]
            a[p, g + 8] = far[np.random.randint(len(far))]
    return np.exp2(a.ravel()).repeat(32)


def f64(x):
    return np.asarray(x).astype(np.float64)


def striped(idx):
    return np.tile(idx.reshape(-1, 16).T, (8, 1)).astype(np.uint16)


def unstriped(offs):
    return offs[:16].T.reshape(-1).astype(np.int64)


E2M1 = np.array([0.0, 0.5, 1.0, 1.5, 2.0, 3.0, 4.0, 6.0, -0.0, -0.5, -1.0, -1.5, -2.0, -3.0, -4.0, -6.0])


def pack_weight(w, fmt):
    k, n = w.shape
    w = f64(np.asarray(w, np.float32).astype(ml_dtypes.bfloat16)).reshape(k // 32, 32, n)
    amax = np.abs(w).max(1)
    if fmt == "e4m3":
        byte = np.frexp(amax)[1] - 1 + 127 - 7
    else:
        mant, ex = np.frexp(amax / 6.0)
        byte = np.where(mant > 0.5, ex, ex - 1) + 127
    byte = np.clip(np.where(amax > 0, byte, 1), 1, 254)
    scaled = (w * np.exp2(127.0 - byte)[:, None, :]).reshape(k, n).astype(np.float32)
    by_word = np.ascontiguousarray(scaled.reshape(k // 512, 128, 4, n).transpose(0, 1, 3, 2))
    if fmt == "e4m3":
        words = by_word.astype(ml_dtypes.float8_e4m3fn).view(np.uint8)
    else:
        c = by_word.astype(ml_dtypes.float4_e2m1fn).view(np.uint8) & 0xF
        words = (c[..., 0::2] | (c[..., 1::2] << 4)).reshape(k // 512, 128, 2 * n)
    return np.ascontiguousarray(words), np.ascontiguousarray(byte.astype(np.uint8).reshape(k // 512, 16, n))


def unpack_weight(words, scales, fmt):
    g, _, n = scales.shape
    words = np.ascontiguousarray(words).reshape(g, 128, n, -1)
    if fmt == "e4m3":
        vals = words.view(ml_dtypes.float8_e4m3fn).astype(np.float64)
    else:
        nib = np.empty((g, 128, n, 4), np.uint8)
        nib[..., 0::2] = words & 0xF
        nib[..., 1::2] = words >> 4
        vals = E2M1[nib]
    vals = vals * np.repeat(np.exp2(scales.astype(np.float64) - 127.0), 8, axis=1)[..., None]
    return vals.transpose(0, 1, 3, 2).reshape(g * 512, n)


def gelu(v):
    return 0.5 * v * (1.0 + np.tanh(np.sqrt(2.0 / np.pi) * (v + 0.044715 * v**3)))


def striped8(idx):
    return np.concatenate([v.reshape(-1, 16).T for v in idx]).astype(np.uint16)


def unstriped8(offs):
    return np.stack([offs[16 * g:16 * g + 16].T.reshape(-1) for g in range(8)]).astype(np.int64)


def heads(h, wgt, idx8):
    r = np.arange(h.shape[0])
    return wgt[r // 4 % 128] * h[r[:, None], idx8[r % 512 // 64]]


K, T, S, P, H, N = 512, 4096, 2048, 1024, 1024, 512

def setup_inputs():
    n = np.random.standard_normal
    s = mx_kscale(K)[:, None]
    u = mx_kscale(H)[:, None]
    tab_words, tab_scales = pack_weight(n((K, T)) * s, "e4m3")
    w1_words, w1_scales = pack_weight(1.5 * n((K, H)) / np.sqrt(K) / s, "e2m1")
    return {
        "tab_words": tab_words, "tab_scales": tab_scales,
        "offs": striped(np.random.permutation(T)[:S]),
        "w1_words": w1_words, "w1_scales": w1_scales,
        "offs2": striped8(np.stack([np.random.permutation(S)[:P] for _ in range(8)])),
        "wgt": np.repeat(np.random.uniform(0.4, 1.0, (8, P)), 16, axis=0).astype(np.float32),
        "c": np.random.uniform(0.05, 0.7, (H, P)).astype(np.float32),
        "gain": (np.exp(0.3 * n(H)) * u[:, 0]).astype(np.float32),
        "w2": (n((H, N)) / np.sqrt(H) / u).astype(np.float32),
        "bias": (0.5 * n(N)).astype(np.float32),
    }

def reference(tab_words, tab_scales, offs, w1_words, w1_scales, offs2, wgt, c, gain, w2, bias):
    v = unpack_weight(tab_words, tab_scales, "e4m3")[:, unstriped(offs)]
    w1 = unpack_weight(w1_words, w1_scales, "e2m1")
    h = 1.0 / (1.0 + np.exp(-(w1.T @ v)))
    x = heads(h, f64(wgt), unstriped8(offs2))
    prior = f64(c)
    z = (x + prior - x * prior) * f64(gain)[:, None]
    y = mxq(f64(w2), 0, "e4m3").T @ mxq(z, 0, "e4m3")
    return y + f64(bias)[:, None]

@@ -1,0 +1,230 @@
+from contextlib import ExitStack
+
+import concourse.mybir as mybir
+
+K, T, S, M, H, N = 512, 4096, 2048, 1024, 1024, 512
+FLOPS = 2 * K * H * S + 2 * H * N * M
+
+F32 = mybir.dt.float32
+BF16 = mybir.dt.bfloat16
+I32 = mybir.dt.int32
+U32 = mybir.dt.uint32
+U16 = mybir.dt.uint16
+U8 = mybir.dt.uint8
+FP8X4 = mybir.dt.float8_e4m3fn_x4
+FP4X4 = mybir.dt.float4_e2m1fn_x4
+ALU = mybir.AluOpType
+ACT = mybir.ActivationFunctionType
+
+P = 128
+PACK = 4
+BANK = 512
+PASSES = H // (P * PACK)
+PLANES = PASSES * PACK
+SLICES = S // BANK
+N_TILES = N // P
+CHUNKS = [(0, 512), (512, 256), (768, 256)]
+
+
+def tile_list_soft_datalog_firing_kernel(
+    tc, tab_words, tab_scales, offs, w1_words, w1_scales, offs2, wgt, c, gain, w2, bias, out
+):
+    nc = tc.nc
+    with ExitStack() as ctx:
+        lists = ctx.enter_context(tc.tile_pool(name="lists", bufs=1))
+        keep = ctx.enter_context(tc.tile_pool(name="keep", bufs=1))
+        ring = ctx.enter_context(tc.tile_pool(name="ring", bufs=1))
+        psum = ctx.enter_context(tc.psum_pool(name="psum", bufs=1))
+
+        facts = lists.tile([P, S // 16], U16, name="facts")
+        atoms = lists.tile([P, M // 16], U16, name="atoms")
+        w1_w = ring.tile([P, H], U16, name="w1_w", tag="slot_a", align_bytes=64)
+        w1_s = ring.tile([P, H], U8, name="w1_s", tag="slot_b", align_bytes=64)
+        tab_s = ring.tile([P, T], U8, name="tab_s", tag="slot_c", align_bytes=64)
+        w1p_w = keep.tile([P, 2 * H], U8, name="w1p_w", align_bytes=64)
+        w1p_s = keep.tile([P, H], U8, name="w1p_s", align_bytes=64)
+        v_w = [keep.tile([P, BANK], U32, name="v_w%d" % s, align_bytes=64) for s in range(SLICES)]
+        v_s = keep.tile([P, S], U8, name="v_s", align_bytes=64)
+        truth = [keep.tile([P, S], F32, name="truth%d" % q) for q in range(PLANES)]
+        w2_w = keep.tile([P, PASSES, N], U32, name="w2_w", align_bytes=64)
+        w2_s = keep.tile([P, PASSES, N], U8, name="w2_s", align_bytes=64)
+        z_w = keep.tile([P, PASSES, M], U32, name="z_w", align_bytes=64)
+        z_s = keep.tile([P, PASSES, M], U8, name="z_s", align_bytes=64)
+        warm = keep.tile([P, 2], F32, name="warm")
+
+        nc.vector.memset(w1_s[:].bitcast(I32), 0)
+        nc.vector.memset(tab_s[:].bitcast(I32), 0)
+        nc.vector.memset(warm[:, 0:1], 0.0)
+        nc.scalar.activation(warm[:, 1:2], warm[:, 0:1], ACT.Sigmoid)
+
+        nc.sync.dma_start(facts[:], offs)
+        nc.sync.dma_start(w1_w[:].bitcast(I32), w1_words[0].bitcast(I32))
+        for q in range(4):
+            nc.sync.dma_start(
+                w1_s[32 * q : 32 * q + 4, :].bitcast(I32), w1_scales[0, 4 * q : 4 * q + 4, :].bitcast(I32)
+            )
+        for q in range(4):
+            nc.sync.dma_start(
+                tab_s[32 * q : 32 * q + 4, :].bitcast(I32), tab_scales[0, 4 * q : 4 * q + 4, :].bitcast(I32)
+            )
+        nc.sync.dma_start(atoms[:], offs2)
+
+        nc.vector.tensor_copy(
+            w1p_w[:].bitcast(U16).rearrange("p (b i m) -> p b i m", b=PASSES, i=PACK),
+            w1_w[:].rearrange("p (b m i) -> p b i m", b=PASSES, i=PACK),
+        )
+        nc.vector.tensor_copy(
+            w1p_s[:].rearrange("p (b i m) -> p b i m", b=PASSES, i=PACK),
+            w1_s[:].rearrange("p (b m i) -> p b i m", b=PASSES, i=PACK),
+        )
+        nc.vector.tensor_copy(v_s[:], tab_s[:].indirect(facts[:]))
+
+        tab_w = ring.tile([P, T], U32, name="tab_w", tag="slot_a", align_bytes=64)
+        nc.sync.dma_start(tab_w[:].bitcast(I32), tab_words[0].rearrange("p t i -> p (t i)").bitcast(I32))
+
+        first = ring.tile([P, (PACK + 1) * M + PLANES], F32, name="first", tag="slot_b", align_bytes=64)
+        wgt_sb = first[:, PACK * M : (PACK + 1) * M]
+        gain_sb = first[:, (PACK + 1) * M :].rearrange("p (b i) -> p b i", i=PACK)
+        c_view = c.rearrange("(b p i) m -> b p i m", p=P, i=PACK)
+        prior = [first[:, 0 : PACK * M].rearrange("p (i m) -> p i m", i=PACK)]
+        nc.sync.dma_start(gain_sb, gain.rearrange("(b p i) -> p b i", p=P, i=PACK))
+        nc.sync.dma_start(prior[0][:, 0, :], c_view[0, :, 0, :])
+        nc.sync.dma_start(wgt_sb, wgt)
+        for i in range(1, PACK):
+            nc.sync.dma_start(prior[0][:, i, :], c_view[0, :, i, :])
+
+        cols = BANK // 16
+        for s in range(SLICES):
+            nc.vector.tensor_copy(v_w[s][:], tab_w[:].indirect(facts[:, s * cols : (s + 1) * cols]))
+
+        w2_view = w2.rearrange("(b p i) n -> b p i n", p=P, i=PACK)
+        second = ring.tile([P, PLANES * N + N_TILES], F32, name="second", tag="slot_c", align_bytes=64)
+        w2_raw = second[:, 0 : PLANES * N].rearrange("p (b i n) -> p b i n", b=PASSES, i=PACK)
+        bias_sb = second[:, PLANES * N :]
+        for b in range(PASSES):
+            nc.sync.dma_start(w2_raw[:, b], w2_view[b])
+        with nc.allow_non_contiguous_dma(reason="one bias value a partition"):
+            nc.sync.dma_start(bias_sb, bias.rearrange("(t p) -> p t", p=P))
+
+        later = ring.tile([P, PACK, M], F32, name="later", tag="slot_a", align_bytes=64)
+        prior.append(later[:])
+        for i in range(PACK):
+            nc.sync.dma_start(prior[1][:, i, :], c_view[1, :, i, :])
+
+        def first_product(q, s):
+            acc = psum.tile([P, BANK], F32, name="acc1", bufs=4)
+            nc.tensor.matmul_mx(
+                out=acc[:],
+                lhsT=w1p_w[:, 2 * P * q : 2 * P * (q + 1)].bitcast(FP4X4),
+                lhsT_scale=w1p_s[:, P * q : P * (q + 1)],
+                rhs=v_w[s][:].bitcast(FP8X4),
+                rhs_scale=v_s[:, s * BANK : (s + 1) * BANK],
+                start=True,
+                stop=True,
+            )
+            nc.scalar.activation(truth[q][:, s * BANK : (s + 1) * BANK], acc[:], ACT.Sigmoid)
+
+        def scale_prior(q):
+            b, i = divmod(q, PACK)
+            nc.scalar.activation(prior[b][:, i, :], prior[b][:, i, :], ACT.Copy, scale=gain_sb[:, b, i : i + 1])
+
+        def slope(q):
+            b, i = divmod(q, PACK)
+            a = ring.tile([P, M], F32, name="slope", bufs=PACK)
+            nc.vector.scalar_tensor_tensor(
+                a[:], prior[b][:, i, :], gain_sb[:, b, i : i + 1], wgt_sb, ALU.subtract, ALU.mult
+            )
+            return a
+
+        def pick(q, a, dst, m0, width):
+            nc.vector.tensor_tensor(
+                dst[:, q % PACK, :],
+                truth[q][:].indirect(atoms[:, m0 // 16 : (m0 + width) // 16]),
+                a[:, m0 : m0 + width],
+                ALU.mult,
+            )
+
+        def join(b, picked, m0, width):
+            z = ring.tile([P, width * PACK], BF16, name="z", bufs=2, align_bytes=64)
+            nc.vector.tensor_tensor(
+                z[:].rearrange("p (c e i) -> p c i e", e=2, i=PACK),
+                prior[b][:, :, m0 : m0 + width].rearrange("p i (c e) -> p c i e", e=2),
+                picked[:].rearrange("p i (c e) -> p c i e", e=2),
+                ALU.subtract,
+            )
+            return z
+
+        def quantise_z(b, z, m0, width):
+            nc.vector.quantize_mx(
+                out=z_w[:, b, m0 : m0 + width].bitcast(FP8X4), scales=z_s[:, b, m0 : m0 + width], in_=z[:]
+            )
+
+        def round_w2(b):
+            g = ring.tile([P, N * PACK], BF16, name="w2_bf", bufs=2, align_bytes=64)
+            nc.scalar.copy(
+                g[:].rearrange("p (c e i) -> p c i e", e=2, i=PACK),
+                w2_raw[:, b].rearrange("p i (c e) -> p c i e", e=2),
+            )
+            return g
+
+        def quantise_w2(b, g):
+            nc.vector.quantize_mx(out=w2_w[:, b, :].bitcast(FP8X4), scales=w2_s[:, b, :], in_=g[:])
+
+        out_view = out.rearrange("(t p) m -> p t m", p=P)
+
+        def second_product(m0, width):
+            res = ring.tile([P, N_TILES, width], F32, name="res", bufs=2)
+            for t in range(N_TILES):
+                acc = psum.tile([P, BANK], F32, name="acc2", bufs=4)
+                for b in range(PASSES):
+                    nc.tensor.matmul_mx(
+                        out=acc[:, 0:width],
+                        lhsT=w2_w[:, b, t * P : (t + 1) * P].bitcast(FP8X4),
+                        lhsT_scale=w2_s[:, b, t * P : (t + 1) * P],
+                        rhs=z_w[:, b, m0 : m0 + width].bitcast(FP8X4),
+                        rhs_scale=z_s[:, b, m0 : m0 + width],
+                        start=(b == 0),
+                        stop=(b == PASSES - 1),
+                    )
+                nc.scalar.activation(res[:, t, :], acc[:, 0:width], ACT.Identity, bias=bias_sb[:, t : t + 1])
+                nc.sync.dma_start(out_view[:, t, m0 : m0 + width], res[:, t, :])
+
+        for s in range(SLICES):
+            first_product(0, s)
+            first_product(1, s)
+            if s == 1:
+                scale_prior(0)
+        scale_prior(1)
+        w2_bf = []
+        for q in range(2, PLANES):
+            for s in range(SLICES):
+                first_product(q, s)
+            scale_prior(q)
+        for b in range(PASSES):
+            w2_bf.append(round_w2(b))
+
+        halves = [ring.tile([P, PACK, BANK], F32, name="picked", bufs=2) for u in range(2)]
+        for q in range(PACK):
+            a = slope(q)
+            for u in range(2):
+                pick(q, a, halves[u], u * BANK, BANK)
+        slopes = [slope(PACK)]
+        zs = [join(0, halves[u], u * BANK, BANK) for u in range(2)]
+        slopes.append(slope(PACK + 1))
+        for u in range(2):
+            quantise_z(0, zs[u], u * BANK, BANK)
+        slopes.append(slope(PACK + 2))
+        slopes.append(slope(PACK + 3))
+        waiting = None
+        for m0, width in CHUNKS:
+            picked = ring.tile([P, PACK, width], F32, name="picked", bufs=2)
+            for i in range(PACK):
+                pick(PACK + i, slopes[i], picked, m0, width)
+                if m0 == 0 and i >= 2:
+                    quantise_w2(i - 2, w2_bf[i - 2])
+                if i == 0 and waiting is not None:
+                    quantise_z(1, waiting[0], waiting[1], waiting[2])
+                    second_product(waiting[1], waiting[2])
+            waiting = (join(1, picked, m0, width), m0, width)
+        quantise_z(1, waiting[0], waiting[1], waiting[2])
+        second_product(waiting[1], waiting[2])

@@ -1,6 +1,7 @@
 from contextlib import ExitStack
 
 import concourse.mybir as mybir
+from concourse.masks import make_identity
 
 K, T, S, M, H, N = 512, 4096, 2048, 1024, 1024, 512
 FLOPS = 2 * K * H * S + 2 * H * N * M
@@ -23,7 +24,9 @@ PASSES = H // (P * PACK)
 PLANES = PASSES * PACK
 SLICES = S // BANK
 N_TILES = N // P
-CHUNKS = [(0, 512), (512, 256), (768, 256)]
+CHUNK = 256
+CHUNKS = M // CHUNK
+TRUTH_BUFS = 6
 
 
 def tile_list_soft_datalog_firing_kernel(
@@ -38,24 +41,28 @@ def tile_list_soft_datalog_firing_kernel(
 
         facts = lists.tile([P, S // 16], U16, name="facts")
         atoms = lists.tile([P, M // 16], U16, name="atoms")
-        w1_w = ring.tile([P, H], U16, name="w1_w", tag="slot_a", align_bytes=64)
+        w1_w = keep.tile([P, H], U16, name="w1_w", align_bytes=64)
         w1_s = ring.tile([P, H], U8, name="w1_s", tag="slot_b", align_bytes=64)
         tab_s = ring.tile([P, T], U8, name="tab_s", tag="slot_c", align_bytes=64)
         w1p_w = keep.tile([P, 2 * H], U8, name="w1p_w", align_bytes=64)
         w1p_s = keep.tile([P, H], U8, name="w1p_s", align_bytes=64)
         v_w = [keep.tile([P, BANK], U32, name="v_w%d" % s, align_bytes=64) for s in range(SLICES)]
         v_s = keep.tile([P, S], U8, name="v_s", align_bytes=64)
-        truth = [keep.tile([P, S], F32, name="truth%d" % q) for q in range(PLANES)]
+        picked = [keep.tile([P, PACK, M], F32, name="picked%d" % b) for b in range(PASSES)]
+        minus_wgt = keep.tile([P, M], F32, name="minus_wgt")
+        ident = keep.tile([P, P], F32, name="ident")
         w2_w = keep.tile([P, PASSES, N], U32, name="w2_w", align_bytes=64)
         w2_s = keep.tile([P, PASSES, N], U8, name="w2_s", align_bytes=64)
         z_w = keep.tile([P, PASSES, M], U32, name="z_w", align_bytes=64)
         z_s = keep.tile([P, PASSES, M], U8, name="z_s", align_bytes=64)
-        warm = keep.tile([P, 2], F32, name="warm")
+        warm = ring.tile([P, 2], F32, name="warm", tag="slot_a", align_bytes=64)
 
+        nc.vector.memset(warm[:, 0:1], 0.0)
         nc.vector.memset(w1_s[:].bitcast(I32), 0)
         nc.vector.memset(tab_s[:].bitcast(I32), 0)
-        nc.vector.memset(warm[:, 0:1], 0.0)
         nc.scalar.activation(warm[:, 1:2], warm[:, 0:1], ACT.Sigmoid)
+
+        make_identity(nc, ident[:])
 
         nc.sync.dma_start(facts[:], offs)
         nc.sync.dma_start(w1_w[:].bitcast(I32), w1_words[0].bitcast(I32))
@@ -93,6 +100,10 @@ def tile_list_soft_datalog_firing_kernel(
         for i in range(1, PACK):
             nc.sync.dma_start(prior[0][:, i, :], c_view[0, :, i, :])
 
+        nc.gpsimd.tensor_scalar(prior[0][:, 0, :], prior[0][:, 0, :], gain_sb[:, 0, 0:1], 0.0, ALU.mult, ALU.add)
+        nc.gpsimd.tensor_scalar(minus_wgt[:], wgt_sb, -1.0, 0.0, ALU.mult, ALU.add)
+        nc.gpsimd.tensor_scalar(prior[0][:, 1, :], prior[0][:, 1, :], gain_sb[:, 0, 1:2], 0.0, ALU.mult, ALU.add)
+
         cols = BANK // 16
         for s in range(SLICES):
             nc.vector.tensor_copy(v_w[s][:], tab_w[:].indirect(facts[:, s * cols : (s + 1) * cols]))
@@ -111,8 +122,12 @@ def tile_list_soft_datalog_firing_kernel(
         for i in range(PACK):
             nc.sync.dma_start(prior[1][:, i, :], c_view[1, :, i, :])
 
+        truth = {}
+
         def first_product(q, s):
-            acc = psum.tile([P, BANK], F32, name="acc1", bufs=4)
+            if s == 0:
+                truth[q] = ring.tile([P, S], F32, name="truth", bufs=TRUTH_BUFS)
+            acc = psum.tile([P, BANK], F32, name="acc", bufs=7)
             nc.tensor.matmul_mx(
                 out=acc[:],
                 lhsT=w1p_w[:, 2 * P * q : 2 * P * (q + 1)].bitcast(FP4X4),
@@ -128,36 +143,66 @@ def tile_list_soft_datalog_firing_kernel(
             b, i = divmod(q, PACK)
             nc.scalar.activation(prior[b][:, i, :], prior[b][:, i, :], ACT.Copy, scale=gain_sb[:, b, i : i + 1])
 
+        slopes = {}
+
         def slope(q):
             b, i = divmod(q, PACK)
-            a = ring.tile([P, M], F32, name="slope", bufs=PACK)
+            slopes[q] = ring.tile([P, M], F32, name="slope", bufs=3)
             nc.vector.scalar_tensor_tensor(
-                a[:], prior[b][:, i, :], gain_sb[:, b, i : i + 1], wgt_sb, ALU.subtract, ALU.mult
+                slopes[q][:], prior[b][:, i, :], gain_sb[:, b, i : i + 1], minus_wgt[:], ALU.subtract, ALU.mult
             )
-            return a
 
-        def pick(q, a, dst, m0, width):
+        def pick(q, m0, m1):
+            b, i = divmod(q, PACK)
             nc.vector.tensor_tensor(
-                dst[:, q % PACK, :],
-                truth[q][:].indirect(atoms[:, m0 // 16 : (m0 + width) // 16]),
-                a[:, m0 : m0 + width],
+                picked[b][:, i, m0:m1],
+                truth[q][:].indirect(atoms[:, m0 // 16 : m1 // 16]),
+                slopes[q][:, m0:m1],
                 ALU.mult,
             )
 
-        def join(b, picked, m0, width):
-            z = ring.tile([P, width * PACK], BF16, name="z", bufs=2, align_bytes=64)
+        def join_on_vector(b, z, m0, width):
             nc.vector.tensor_tensor(
-                z[:].rearrange("p (c e i) -> p c i e", e=2, i=PACK),
+                z.rearrange("p (c e i) -> p c i e", e=2, i=PACK),
                 prior[b][:, :, m0 : m0 + width].rearrange("p i (c e) -> p c i e", e=2),
-                picked[:].rearrange("p i (c e) -> p c i e", e=2),
-                ALU.subtract,
+                picked[b][:, :, m0 : m0 + width].rearrange("p i (c e) -> p c i e", e=2),
+                ALU.add,
             )
-            return z
 
-        def quantise_z(b, z, m0, width):
-            nc.vector.quantize_mx(
-                out=z_w[:, b, m0 : m0 + width].bitcast(FP8X4), scales=z_s[:, b, m0 : m0 + width], in_=z[:]
+        def join_on_tensor(b, z, m0, width):
+            back = psum.tile([P, width // P, 2, P], F32, name="back", bufs=1)
+            for k in range(width // P):
+                block = slice(m0 + k * P, m0 + (k + 1) * P)
+                turned = psum.tile([P, PACK, P], F32, name="turned", tag="acc", bufs=7)
+                for i in range(PACK):
+                    nc.tensor.matmul(
+                        turned[:, i, :], prior[b][:, i, block], ident[:], start=True, stop=False, is_transpose=True
+                    )
+                    nc.tensor.matmul(
+                        turned[:, i, :], picked[b][:, i, block], ident[:], start=False, stop=True, is_transpose=True
+                    )
+                rounded = ring.tile([P, PACK * P], BF16, name="rounded", bufs=2)
+                nc.scalar.copy(
+                    rounded[:].rearrange("m (u p e) -> m u p e", u=2, e=2),
+                    turned[:].rearrange("m (u e) p -> m u p e", u=2),
+                )
+                pairs = rounded[:].bitcast(F32)
+                for u in range(2):
+                    nc.tensor.transpose(back[:, k, u, :], pairs[:, u * P : (u + 1) * P], ident[:])
+            nc.scalar.copy(
+                z.bitcast(F32).rearrange("p (k m u) -> p k m u", u=2, m=P),
+                back[:].rearrange("p k u m -> p k m u"),
             )
+
+        zs = {}
+
+        def join(how, b, m0, width):
+            zs[b, m0] = ring.tile([P, width * PACK], BF16, name="z", bufs=9, align_bytes=64)
+            how(b, zs[b, m0][:], m0, width)
+
+        def quantise_z(b, m0, width):
+            cols = slice(m0, m0 + width)
+            nc.vector.quantize_mx(out=z_w[:, b, cols].bitcast(FP8X4), scales=z_s[:, b, cols], in_=zs[b, m0][:])
 
         def round_w2(b):
             g = ring.tile([P, N * PACK], BF16, name="w2_bf", bufs=2, align_bytes=64)
@@ -172,59 +217,100 @@ def tile_list_soft_datalog_firing_kernel(
 
         out_view = out.rearrange("(t p) m -> p t m", p=P)
 
-        def second_product(m0, width):
-            res = ring.tile([P, N_TILES, width], F32, name="res", bufs=2)
+        banks = {}
+
+        def second_product(b, m0, width):
+            cols = slice(m0, m0 + width)
             for t in range(N_TILES):
-                acc = psum.tile([P, BANK], F32, name="acc2", bufs=4)
-                for b in range(PASSES):
-                    nc.tensor.matmul_mx(
-                        out=acc[:, 0:width],
-                        lhsT=w2_w[:, b, t * P : (t + 1) * P].bitcast(FP8X4),
-                        lhsT_scale=w2_s[:, b, t * P : (t + 1) * P],
-                        rhs=z_w[:, b, m0 : m0 + width].bitcast(FP8X4),
-                        rhs_scale=z_s[:, b, m0 : m0 + width],
-                        start=(b == 0),
-                        stop=(b == PASSES - 1),
+                u, half = divmod(t, 2)
+                if b == 0 and half == 0:
+                    banks[m0, u] = psum.tile([P, 2, width], F32, name="evidence", tag="acc", bufs=7)
+                nc.tensor.matmul_mx(
+                    out=banks[m0, u][:, half, :],
+                    lhsT=w2_w[:, b, t * P : (t + 1) * P].bitcast(FP8X4),
+                    lhsT_scale=w2_s[:, b, t * P : (t + 1) * P],
+                    rhs=z_w[:, b, cols].bitcast(FP8X4),
+                    rhs_scale=z_s[:, b, cols],
+                    start=(b == 0 and half == 0),
+                    stop=(b == PASSES - 1 and half == 1),
+                )
+
+        def store(m0, width):
+            res = ring.tile([P, N_TILES, width], F32, name="res", bufs=5)
+            for t in range(N_TILES):
+                u, half = divmod(t, 2)
+                if u == 0 or width == CHUNK:
+                    nc.scalar.activation(
+                        res[:, t, :], banks[m0, u][:, half, :], ACT.Identity, bias=bias_sb[:, t : t + 1]
                     )
-                nc.scalar.activation(res[:, t, :], acc[:, 0:width], ACT.Identity, bias=bias_sb[:, t : t + 1])
-                nc.sync.dma_start(out_view[:, t, m0 : m0 + width], res[:, t, :])
+                else:
+                    nc.vector.tensor_scalar(
+                        res[:, t, :], banks[m0, u][:, half, :], bias_sb[:, t : t + 1], None, ALU.add
+                    )
+                if half == 1:
+                    nc.sync.dma_start(out_view[:, t - 1 : t + 1, m0 : m0 + width], res[:, t - 1 : t + 1, :])
 
         for s in range(SLICES):
             first_product(0, s)
             first_product(1, s)
-            if s == 1:
-                scale_prior(0)
-        scale_prior(1)
+            if s in (1, 3):
+                slope(s // 2)
+        pick(0, 0, M)
+        scale_prior(2)
+        slope(2)
+        pick(1, 0, M)
+        last = PLANES - 1
+        chunk = [(j * CHUNK, CHUNK) for j in range(CHUNKS)]
         w2_bf = []
-        for q in range(2, PLANES):
+        for q in range(2, last):
             for s in range(SLICES):
                 first_product(q, s)
-            scale_prior(q)
-        for b in range(PASSES):
-            w2_bf.append(round_w2(b))
+            scale_prior(q + 1)
+            slope(q + 1)
+            pick(q, 0, M)
+            if q == PACK - 1:
+                w2_bf.append(round_w2(0))
+            if q == PACK:
+                quantise_w2(0, w2_bf[0])
+                join(join_on_vector, 0, *chunk[1])
+            if q == PACK + 1:
+                join(join_on_tensor, 0, *chunk[0])
+                quantise_z(0, *chunk[1])
+            if q == PACK + 2:
+                w2_bf.append(round_w2(1))
+                quantise_z(0, *chunk[0])
+        for s in range(SLICES):
+            first_product(last, s)
+        second_product(0, *chunk[0])
+        join(join_on_tensor, 0, *chunk[2])
+        second_product(0, *chunk[1])
 
-        halves = [ring.tile([P, PACK, BANK], F32, name="picked", bufs=2) for u in range(2)]
-        for q in range(PACK):
-            a = slope(q)
-            for u in range(2):
-                pick(q, a, halves[u], u * BANK, BANK)
-        slopes = [slope(PACK)]
-        zs = [join(0, halves[u], u * BANK, BANK) for u in range(2)]
-        slopes.append(slope(PACK + 1))
-        for u in range(2):
-            quantise_z(0, zs[u], u * BANK, BANK)
-        slopes.append(slope(PACK + 2))
-        slopes.append(slope(PACK + 3))
-        waiting = None
-        for m0, width in CHUNKS:
-            picked = ring.tile([P, PACK, width], F32, name="picked", bufs=2)
-            for i in range(PACK):
-                pick(PACK + i, slopes[i], picked, m0, width)
-                if m0 == 0 and i >= 2:
-                    quantise_w2(i - 2, w2_bf[i - 2])
-                if i == 0 and waiting is not None:
-                    quantise_z(1, waiting[0], waiting[1], waiting[2])
-                    second_product(waiting[1], waiting[2])
-            waiting = (join(1, picked, m0, width), m0, width)
-        quantise_z(1, waiting[0], waiting[1], waiting[2])
-        second_product(waiting[1], waiting[2])
+        def pick_last(m0, width):
+            pick(last, m0, m0 + width)
+
+        def finish(m0, width):
+            quantise_z(1, m0, width)
+            second_product(1, m0, width)
+            store(m0, width)
+
+        pick_last(*chunk[0])
+        quantise_w2(1, w2_bf[1])
+        join(join_on_vector, 1, *chunk[0])
+        pick_last(*chunk[1])
+        finish(*chunk[0])
+        join(join_on_tensor, 0, *chunk[3])
+        join(join_on_vector, 1, *chunk[1])
+        pick_last(*chunk[2])
+        finish(*chunk[1])
+        join(join_on_vector, 1, *chunk[2])
+        quantise_z(0, *chunk[2])
+        second_product(0, *chunk[2])
+        pick_last(*chunk[3])
+        finish(*chunk[2])
+        quantise_z(0, *chunk[3])
+        halves = [(chunk[3][0] + h * P, P) for h in range(2)]
+        for piece in halves:
+            second_product(0, *piece)
+            join(join_on_vector, 1, *piece)
+        for piece in halves:
+            finish(*piece)

@@ -26,7 +26,8 @@ SLICES = S // BANK
 N_TILES = N // P
 CHUNK = 256
 CHUNKS = M // CHUNK
-TRUTH_BUFS = 6
+ACC_BANKS = 6
+EARLY = 2
 
 
 def tile_list_soft_datalog_firing_kernel(
@@ -48,8 +49,6 @@ def tile_list_soft_datalog_firing_kernel(
         w1p_s = keep.tile([P, H], U8, name="w1p_s", align_bytes=64)
         v_w = [keep.tile([P, BANK], U32, name="v_w%d" % s, align_bytes=64) for s in range(SLICES)]
         v_s = keep.tile([P, S], U8, name="v_s", align_bytes=64)
-        picked = [keep.tile([P, PACK, M], F32, name="picked%d" % b) for b in range(PASSES)]
-        minus_wgt = keep.tile([P, M], F32, name="minus_wgt")
         ident = keep.tile([P, P], F32, name="ident")
         w2_w = keep.tile([P, PASSES, N], U32, name="w2_w", align_bytes=64)
         w2_s = keep.tile([P, PASSES, N], U8, name="w2_s", align_bytes=64)
@@ -89,45 +88,56 @@ def tile_list_soft_datalog_firing_kernel(
         tab_w = ring.tile([P, T], U32, name="tab_w", tag="slot_a", align_bytes=64)
         nc.sync.dma_start(tab_w[:].bitcast(I32), tab_words[0].rearrange("p t i -> p (t i)").bitcast(I32))
 
-        first = ring.tile([P, (PACK + 1) * M + PLANES], F32, name="first", tag="slot_b", align_bytes=64)
-        wgt_sb = first[:, PACK * M : (PACK + 1) * M]
-        gain_sb = first[:, (PACK + 1) * M :].rearrange("p (b i) -> p b i", i=PACK)
+        early = ring.tile([P, PLANES + (1 + EARLY) * M], F32, name="early", tag="slot_b", align_bytes=64)
+        gain_sb = early[:, 0:PLANES]
+        minus_wgt = early[:, PLANES : PLANES + M]
         c_view = c.rearrange("(b p i) m -> b p i m", p=P, i=PACK)
-        prior = [first[:, 0 : PACK * M].rearrange("p (i m) -> p i m", i=PACK)]
-        nc.sync.dma_start(gain_sb, gain.rearrange("(b p i) -> p b i", p=P, i=PACK))
-        nc.sync.dma_start(prior[0][:, 0, :], c_view[0, :, 0, :])
-        nc.sync.dma_start(wgt_sb, wgt)
-        for i in range(1, PACK):
-            nc.sync.dma_start(prior[0][:, i, :], c_view[0, :, i, :])
+        w2_view = w2.rearrange("(b p i) n -> b p i n", p=P, i=PACK)
+        prior = [early[:, PLANES + (1 + q) * M : PLANES + (2 + q) * M] for q in range(EARLY)]
 
-        nc.gpsimd.tensor_scalar(prior[0][:, 0, :], prior[0][:, 0, :], gain_sb[:, 0, 0:1], 0.0, ALU.mult, ALU.add)
-        nc.gpsimd.tensor_scalar(minus_wgt[:], wgt_sb, -1.0, 0.0, ALU.mult, ALU.add)
-        nc.gpsimd.tensor_scalar(prior[0][:, 1, :], prior[0][:, 1, :], gain_sb[:, 0, 1:2], 0.0, ALU.mult, ALU.add)
+        nc.sync.dma_start(
+            gain_sb.rearrange("p (b i) -> p b i", i=PACK), gain.rearrange("(b p i) -> p b i", p=P, i=PACK)
+        )
+        nc.sync.dma_start(prior[0], c_view[0, :, 0, :])
+        nc.sync.dma_start(minus_wgt, wgt)
+        for q in range(1, EARLY):
+            nc.sync.dma_start(prior[q], c_view[0, :, q, :])
+
+        late = ring.tile([P, 2 * M + PLANES * N + N_TILES], F32, name="late", tag="slot_c", align_bytes=64)
+        prior.extend([late[:, q * M : (q + 1) * M] for q in range(2)])
+        w2_raw = late[:, 2 * M : 2 * M + PLANES * N].rearrange("p (b i n) -> p b i n", b=PASSES, i=PACK)
+        bias_sb = late[:, 2 * M + PLANES * N :]
+        for q in range(EARLY, PACK):
+            nc.sync.dma_start(prior[q], c_view[0, :, q, :])
+        for b in range(PASSES):
+            nc.sync.dma_start(w2_raw[:, b], w2_view[b])
+        with nc.allow_non_contiguous_dma(reason="one bias value a partition"):
+            nc.sync.dma_start(bias_sb, bias.rearrange("(t p) -> p t", p=P))
+        prior1 = keep.tile([P, PACK, M], F32, name="prior1")
+        prior.extend([prior1[:, i, :] for i in range(PACK)])
+
+        def prior_on_gpsimd(q, raw):
+            nc.gpsimd.tensor_scalar(prior[q], raw, gain_sb[:, q : q + 1], 0.0, ALU.mult, ALU.add)
+
+        prior_on_gpsimd(0, prior[0])
+        nc.gpsimd.tensor_scalar(minus_wgt, minus_wgt, -1.0, 0.0, ALU.mult, ALU.add)
+        prior_on_gpsimd(1, prior[1])
 
         cols = BANK // 16
         for s in range(SLICES):
             nc.vector.tensor_copy(v_w[s][:], tab_w[:].indirect(facts[:, s * cols : (s + 1) * cols]))
 
-        w2_view = w2.rearrange("(b p i) n -> b p i n", p=P, i=PACK)
-        second = ring.tile([P, PLANES * N + N_TILES], F32, name="second", tag="slot_c", align_bytes=64)
-        w2_raw = second[:, 0 : PLANES * N].rearrange("p (b i n) -> p b i n", b=PASSES, i=PACK)
-        bias_sb = second[:, PLANES * N :]
-        for b in range(PASSES):
-            nc.sync.dma_start(w2_raw[:, b], w2_view[b])
-        with nc.allow_non_contiguous_dma(reason="one bias value a partition"):
-            nc.sync.dma_start(bias_sb, bias.rearrange("(t p) -> p t", p=P))
-
-        later = ring.tile([P, PACK, M], F32, name="later", tag="slot_a", align_bytes=64)
-        prior.append(later[:])
-        for i in range(PACK):
-            nc.sync.dma_start(prior[1][:, i, :], c_view[1, :, i, :])
+        res = ring.tile([P, N_TILES, M], F32, name="res", tag="slot_a", align_bytes=64)
 
         truth = {}
 
+        def bank(name):
+            return psum.tile([P, BANK], F32, name=name, tag="acc", bufs=ACC_BANKS)
+
         def first_product(q, s):
             if s == 0:
-                truth[q] = ring.tile([P, S], F32, name="truth", bufs=TRUTH_BUFS)
-            acc = psum.tile([P, BANK], F32, name="acc", bufs=7)
+                truth[q] = ring.tile([P, S], F32, name="truth", tag="window%d" % q)
+            acc = bank("acc")
             nc.tensor.matmul_mx(
                 out=acc[:],
                 lhsT=w1p_w[:, 2 * P * q : 2 * P * (q + 1)].bitcast(FP4X4),
@@ -139,81 +149,131 @@ def tile_list_soft_datalog_firing_kernel(
             )
             nc.scalar.activation(truth[q][:, s * BANK : (s + 1) * BANK], acc[:], ACT.Sigmoid)
 
-        def scale_prior(q):
-            b, i = divmod(q, PACK)
-            nc.scalar.activation(prior[b][:, i, :], prior[b][:, i, :], ACT.Copy, scale=gain_sb[:, b, i : i + 1])
+        def truth_plane(q):
+            for s in range(SLICES):
+                first_product(q, s)
+
+        wgt_ps = [psum.tile([P, BANK], F32, name="wgt_ps", tag="wgt_ps%d" % h) for h in range(M // BANK)]
+
+        def wgt_to_psum():
+            for h in range(M // BANK):
+                turned = bank("wgt_turned")
+                for k in range(PACK):
+                    m0 = h * BANK + k * P
+                    nc.tensor.transpose(turned[:, k * P : (k + 1) * P], minus_wgt[:, m0 : m0 + P], ident[:])
+                across = ring.tile([P, BANK], F32, name="across", tag="rounded%d" % h)
+                nc.scalar.copy(across[:], turned[:])
+                for k in range(PACK):
+                    nc.tensor.transpose(wgt_ps[h][:, k * P : (k + 1) * P], across[:, k * P : (k + 1) * P], ident[:])
 
         slopes = {}
 
-        def slope(q):
-            b, i = divmod(q, PACK)
-            slopes[q] = ring.tile([P, M], F32, name="slope", bufs=3)
-            nc.vector.scalar_tensor_tensor(
-                slopes[q][:], prior[b][:, i, :], gain_sb[:, b, i : i + 1], minus_wgt[:], ALU.subtract, ALU.mult
-            )
+        def slope_tag(q):
+            return "slope%d" % q if q < EARLY else "window%d" % (q - 2)
 
-        def pick(q, m0, m1):
-            b, i = divmod(q, PACK)
+        def slope(q):
+            slopes[q] = ring.tile([P, M], F32, name="slope", tag=slope_tag(q))
+            if q < EARLY:
+                nc.vector.scalar_tensor_tensor(
+                    slopes[q][:], prior[q], gain_sb[:, q : q + 1], minus_wgt, ALU.subtract, ALU.mult
+                )
+            else:
+                for h in range(M // BANK):
+                    half = slice(h * BANK, (h + 1) * BANK)
+                    nc.vector.scalar_tensor_tensor(
+                        slopes[q][:, half],
+                        prior[q][:, half],
+                        gain_sb[:, q : q + 1],
+                        wgt_ps[h][:],
+                        ALU.subtract,
+                        ALU.mult,
+                    )
+
+        def late_prior(q):
+            raw = ring.tile([P, M], F32, name="raw", tag=slope_tag(q - PACK))
+            nc.sync.dma_start(raw[:], c_view[1, :, q - PACK, :])
+            prior_on_gpsimd(q, raw[:])
+
+        pairs0 = [ring.tile([P, 2, M], F32, name="picked0", tag="pair%d" % u, align_bytes=64) for u in range(2)]
+        picked1 = keep.tile([P, PACK, M], F32, name="picked1")
+        picked = [pairs0[q // 2][:, q % 2, :] for q in range(PACK)] + [picked1[:, i, :] for i in range(PACK)]
+
+        def pick(q, m0=0, width=M):
             nc.vector.tensor_tensor(
-                picked[b][:, i, m0:m1],
-                truth[q][:].indirect(atoms[:, m0 // 16 : m1 // 16]),
-                slopes[q][:, m0:m1],
+                picked[q][:, m0 : m0 + width],
+                truth[q][:].indirect(atoms[:, m0 // 16 : (m0 + width) // 16]),
+                slopes[q][:, m0 : m0 + width],
                 ALU.mult,
             )
 
-        def join_on_vector(b, z, m0, width):
-            nc.vector.tensor_tensor(
-                z.rearrange("p (c e i) -> p c i e", e=2, i=PACK),
-                prior[b][:, :, m0 : m0 + width].rearrange("p i (c e) -> p c i e", e=2),
-                picked[b][:, :, m0 : m0 + width].rearrange("p i (c e) -> p c i e", e=2),
-                ALU.add,
-            )
+        rounded = {}
 
-        def join_on_tensor(b, z, m0, width):
-            back = psum.tile([P, width // P, 2, P], F32, name="back", bufs=1)
-            for k in range(width // P):
-                block = slice(m0 + k * P, m0 + (k + 1) * P)
-                turned = psum.tile([P, PACK, P], F32, name="turned", tag="acc", bufs=7)
-                for i in range(PACK):
+        def new_rounded(g):
+            rounded[g] = ring.tile([P, 2 * M if g < 2 else M], BF16, name="rounded", tag="rounded%d" % g)
+
+        def forward(g, j):
+            turned = bank("turned")
+            for k in range(CHUNK // P):
+                m0 = j * CHUNK + k * P
+                for e in range(2):
+                    dst = turned[:, (2 * k + e) * P : (2 * k + e + 1) * P]
                     nc.tensor.matmul(
-                        turned[:, i, :], prior[b][:, i, block], ident[:], start=True, stop=False, is_transpose=True
+                        dst, prior[2 * g + e][:, m0 : m0 + P], ident[:], start=True, stop=False, is_transpose=True
                     )
                     nc.tensor.matmul(
-                        turned[:, i, :], picked[b][:, i, block], ident[:], start=False, stop=True, is_transpose=True
+                        dst, picked[2 * g + e][:, m0 : m0 + P], ident[:], start=False, stop=True, is_transpose=True
                     )
-                rounded = ring.tile([P, PACK * P], BF16, name="rounded", bufs=2)
-                nc.scalar.copy(
-                    rounded[:].rearrange("m (u p e) -> m u p e", u=2, e=2),
-                    turned[:].rearrange("m (u e) p -> m u p e", u=2),
-                )
-                pairs = rounded[:].bitcast(F32)
-                for u in range(2):
-                    nc.tensor.transpose(back[:, k, u, :], pairs[:, u * P : (u + 1) * P], ident[:])
             nc.scalar.copy(
-                z.bitcast(F32).rearrange("p (k m u) -> p k m u", u=2, m=P),
-                back[:].rearrange("p k u m -> p k m u"),
+                rounded[g][:, 2 * j * CHUNK : 2 * (j + 1) * CHUNK].rearrange("m (k p e) -> m k p e", k=2, e=2),
+                turned[:].rearrange("m (k e p) -> m k p e", k=2, e=2),
             )
 
         zs = {}
 
-        def join(how, b, m0, width):
-            zs[b, m0] = ring.tile([P, width * PACK], BF16, name="z", bufs=9, align_bytes=64)
-            how(b, zs[b, m0][:], m0, width)
+        def new_z(b):
+            zs[b] = ring.tile([P, PACK * M], BF16, name="z", tag="pair%d" % b, align_bytes=64)
+
+        def backward(b, j):
+            back = bank("back")[:].rearrange("p (k u m) -> p k u m", u=2, m=P)
+            for k in range(CHUNK // P):
+                m0 = j * CHUNK + k * P
+                for u in range(2):
+                    words = rounded[2 * b + u][:].bitcast(F32)
+                    nc.tensor.transpose(back[:, k, u, :], words[:, m0 : m0 + P], ident[:])
+            nc.scalar.copy(
+                zs[b][:, PACK * j * CHUNK : PACK * (j + 1) * CHUNK]
+                .bitcast(F32)
+                .rearrange("p (k m u) -> p k m u", u=2, m=P),
+                back.rearrange("p k u m -> p k m u"),
+            )
+
+        def join_on_vector(m0, width):
+            nc.vector.tensor_tensor(
+                zs[1][:, PACK * m0 : PACK * (m0 + width)].rearrange("p (c e i) -> p c i e", e=2, i=PACK),
+                prior1[:, :, m0 : m0 + width].rearrange("p i (c e) -> p c i e", e=2),
+                picked1[:, :, m0 : m0 + width].rearrange("p i (c e) -> p c i e", e=2),
+                ALU.add,
+            )
 
         def quantise_z(b, m0, width):
             cols = slice(m0, m0 + width)
-            nc.vector.quantize_mx(out=z_w[:, b, cols].bitcast(FP8X4), scales=z_s[:, b, cols], in_=zs[b, m0][:])
+            nc.vector.quantize_mx(
+                out=z_w[:, b, cols].bitcast(FP8X4),
+                scales=z_s[:, b, cols],
+                in_=zs[b][:, PACK * m0 : PACK * (m0 + width)],
+            )
+
+        w2_bf = {}
 
         def round_w2(b):
-            g = ring.tile([P, N * PACK], BF16, name="w2_bf", bufs=2, align_bytes=64)
+            w2_bf[b] = ring.tile([P, N * PACK], BF16, name="w2_bf", bufs=2, align_bytes=64)
             nc.scalar.copy(
-                g[:].rearrange("p (c e i) -> p c i e", e=2, i=PACK),
+                w2_bf[b][:].rearrange("p (c e i) -> p c i e", e=2, i=PACK),
                 w2_raw[:, b].rearrange("p i (c e) -> p c i e", e=2),
             )
-            return g
 
-        def quantise_w2(b, g):
-            nc.vector.quantize_mx(out=w2_w[:, b, :].bitcast(FP8X4), scales=w2_s[:, b, :], in_=g[:])
+        def quantise_w2(b):
+            nc.vector.quantize_mx(out=w2_w[:, b, :].bitcast(FP8X4), scales=w2_s[:, b, :], in_=w2_bf[b][:])
 
         out_view = out.rearrange("(t p) m -> p t m", p=P)
 
@@ -224,7 +284,7 @@ def tile_list_soft_datalog_firing_kernel(
             for t in range(N_TILES):
                 u, half = divmod(t, 2)
                 if b == 0 and half == 0:
-                    banks[m0, u] = psum.tile([P, 2, width], F32, name="evidence", tag="acc", bufs=7)
+                    banks[m0, u] = psum.tile([P, 2, width], F32, name="evidence", tag="acc", bufs=ACC_BANKS)
                 nc.tensor.matmul_mx(
                     out=banks[m0, u][:, half, :],
                     lhsT=w2_w[:, b, t * P : (t + 1) * P].bitcast(FP8X4),
@@ -235,82 +295,103 @@ def tile_list_soft_datalog_firing_kernel(
                     stop=(b == PASSES - 1 and half == 1),
                 )
 
-        def store(m0, width):
-            res = ring.tile([P, N_TILES, width], F32, name="res", bufs=5)
+        def store(m0, width, shared):
+            cols = slice(m0, m0 + width)
             for t in range(N_TILES):
                 u, half = divmod(t, 2)
-                if u == 0 or width == CHUNK:
+                if u == 0 or not shared:
                     nc.scalar.activation(
-                        res[:, t, :], banks[m0, u][:, half, :], ACT.Identity, bias=bias_sb[:, t : t + 1]
+                        res[:, t, cols], banks[m0, u][:, half, :], ACT.Identity, bias=bias_sb[:, t : t + 1]
                     )
                 else:
                     nc.vector.tensor_scalar(
-                        res[:, t, :], banks[m0, u][:, half, :], bias_sb[:, t : t + 1], None, ALU.add
+                        res[:, t, cols], banks[m0, u][:, half, :], bias_sb[:, t : t + 1], None, ALU.add
                     )
                 if half == 1:
-                    nc.sync.dma_start(out_view[:, t - 1 : t + 1, m0 : m0 + width], res[:, t - 1 : t + 1, :])
+                    nc.sync.dma_start(out_view[:, t - 1 : t + 1, cols], res[:, t - 1 : t + 1, cols])
+
+        def both_products(m0, width):
+            second_product(0, m0, width)
+            second_product(1, m0, width)
 
         for s in range(SLICES):
             first_product(0, s)
             first_product(1, s)
             if s in (1, 3):
                 slope(s // 2)
-        pick(0, 0, M)
-        scale_prior(2)
+        nc.scalar.activation(prior[2], prior[2], ACT.Copy, scale=gain_sb[:, 2:3])
+        wgt_to_psum()
+        pick(0)
+        prior_on_gpsimd(3, prior[3])
+        late_prior(4)
         slope(2)
-        pick(1, 0, M)
-        last = PLANES - 1
-        chunk = [(j * CHUNK, CHUNK) for j in range(CHUNKS)]
-        w2_bf = []
-        for q in range(2, last):
-            for s in range(SLICES):
-                first_product(q, s)
-            scale_prior(q + 1)
-            slope(q + 1)
-            pick(q, 0, M)
-            if q == PACK - 1:
-                w2_bf.append(round_w2(0))
-            if q == PACK:
-                quantise_w2(0, w2_bf[0])
-                join(join_on_vector, 0, *chunk[1])
-            if q == PACK + 1:
-                join(join_on_tensor, 0, *chunk[0])
-                quantise_z(0, *chunk[1])
-            if q == PACK + 2:
-                w2_bf.append(round_w2(1))
-                quantise_z(0, *chunk[0])
-        for s in range(SLICES):
-            first_product(last, s)
-        second_product(0, *chunk[0])
-        join(join_on_tensor, 0, *chunk[2])
-        second_product(0, *chunk[1])
+        truth_plane(2)
+        pick(1)
+        late_prior(5)
+        slope(3)
+        truth_plane(3)
+        pick(2)
+        late_prior(6)
+        slope(4)
 
-        def pick_last(m0, width):
-            pick(last, m0, m0 + width)
+        def plane_with_forward(q, g, j):
+            for half in range(2):
+                forward(g, j + half)
+                first_product(q, 2 * half)
+                first_product(q, 2 * half + 1)
 
-        def finish(m0, width):
-            quantise_z(1, m0, width)
-            second_product(1, m0, width)
-            store(m0, width)
-
-        pick_last(*chunk[0])
-        quantise_w2(1, w2_bf[1])
-        join(join_on_vector, 1, *chunk[0])
-        pick_last(*chunk[1])
-        finish(*chunk[0])
-        join(join_on_tensor, 0, *chunk[3])
-        join(join_on_vector, 1, *chunk[1])
-        pick_last(*chunk[2])
-        finish(*chunk[1])
-        join(join_on_vector, 1, *chunk[2])
-        quantise_z(0, *chunk[2])
-        second_product(0, *chunk[2])
-        pick_last(*chunk[3])
-        finish(*chunk[2])
-        quantise_z(0, *chunk[3])
-        halves = [(chunk[3][0] + h * P, P) for h in range(2)]
-        for piece in halves:
-            second_product(0, *piece)
-            join(join_on_vector, 1, *piece)
-        for piece in halves:
-            finish(*piece)
+        new_rounded(0)
+        plane_with_forward(4, 0, 0)
+        pick(3)
+        late_prior(7)
+        slope(5)
+        plane_with_forward(5, 0, 2)
+        pick(4)
+        round_w2(0)
+        slope(6)
+        new_rounded(1)
+        plane_with_forward(6, 1, 0)
+        pick(5)
+        quantise_w2(0)
+        slope(7)
+        plane_with_forward(7, 1, 2)
+        pick(6)
+        new_z(0)
+        new_z(1)
+        new_rounded(2)
+        new_rounded(3)
+        round_w2(1)
+        pick(7, 0, CHUNK)
+        pick(7, CHUNK, CHUNK)
+        backward(0, 1)
+        backward(0, 2)
+        forward(2, 0)
+        forward(3, 0)
+        join_on_vector(CHUNK, CHUNK)
+        quantise_w2(1)
+        quantise_z(0, CHUNK, CHUNK)
+        quantise_z(1, CHUNK, CHUNK)
+        pick(7, 2 * CHUNK, CHUNK)
+        both_products(CHUNK, CHUNK)
+        backward(0, 0)
+        join_on_vector(2 * CHUNK, CHUNK)
+        quantise_z(0, 2 * CHUNK, CHUNK)
+        store(CHUNK, CHUNK, False)
+        backward(1, 0)
+        backward(0, 3)
+        quantise_z(1, 2 * CHUNK, CHUNK)
+        pick(7, 3 * CHUNK, CHUNK)
+        both_products(2 * CHUNK, CHUNK)
+        quantise_z(0, 0, CHUNK)
+        quantise_z(1, 0, CHUNK)
+        store(2 * CHUNK, CHUNK, False)
+        both_products(0, CHUNK)
+        quantise_z(0, 3 * CHUNK, CHUNK)
+        for h in range(2):
+            join_on_vector(3 * CHUNK + h * P, P)
+            second_product(0, 3 * CHUNK + h * P, P)
+        store(0, CHUNK, False)
+        for h in range(2):
+            quantise_z(1, 3 * CHUNK + h * P, P)
+            second_product(1, 3 * CHUNK + h * P, P)
+            store(3 * CHUNK + h * P, P, True)

@@ -42,51 +42,53 @@ def tile_list_soft_datalog_firing_kernel(
 
         facts = lists.tile([P, S // 16], U16, name="facts")
         atoms = lists.tile([P, M // 16], U16, name="atoms")
-        w1_w = keep.tile([P, H], U16, name="w1_w", align_bytes=64)
-        w1_s = ring.tile([P, H], U8, name="w1_s", tag="slot_b", align_bytes=64)
+        w1_w = ring.tile([P, H], U16, name="w1_w", tag="slot_b", align_bytes=64)
+        w1_s = ring.tile([P, H], U8, name="w1_s", tag="slot_d", align_bytes=64)
         tab_s = ring.tile([P, T], U8, name="tab_s", tag="slot_c", align_bytes=64)
         w1p_w = keep.tile([P, 2 * H], U8, name="w1p_w", align_bytes=64)
         w1p_s = keep.tile([P, H], U8, name="w1p_s", align_bytes=64)
-        v_w = [keep.tile([P, BANK], U32, name="v_w%d" % s, align_bytes=64) for s in range(SLICES)]
         v_s = keep.tile([P, S], U8, name="v_s", align_bytes=64)
         ident = keep.tile([P, P], F32, name="ident")
         w2_w = keep.tile([P, PASSES, N], U32, name="w2_w", align_bytes=64)
         w2_s = keep.tile([P, PASSES, N], U8, name="w2_s", align_bytes=64)
         z_w = keep.tile([P, PASSES, M], U32, name="z_w", align_bytes=64)
         z_s = keep.tile([P, PASSES, M], U8, name="z_s", align_bytes=64)
-        warm = ring.tile([P, 2], F32, name="warm", tag="slot_a", align_bytes=64)
+        warm = keep.tile([P, 2], F32, name="warm")
+        zeros = ring.tile([P, H // 4], I32, name="zeros", tag="slot_a", align_bytes=64)
 
         nc.vector.memset(warm[:, 0:1], 0.0)
-        nc.vector.memset(w1_s[:].bitcast(I32), 0)
         nc.vector.memset(tab_s[:].bitcast(I32), 0)
+        nc.vector.memset(zeros[:], 0)
+        nc.vector.tensor_copy(w1_s[:].bitcast(I32), zeros[:])
         nc.scalar.activation(warm[:, 1:2], warm[:, 0:1], ACT.Sigmoid)
 
         make_identity(nc, ident[:])
 
-        nc.sync.dma_start(facts[:], offs)
         nc.sync.dma_start(w1_w[:].bitcast(I32), w1_words[0].bitcast(I32))
-        for q in range(4):
-            nc.sync.dma_start(
-                w1_s[32 * q : 32 * q + 4, :].bitcast(I32), w1_scales[0, 4 * q : 4 * q + 4, :].bitcast(I32)
-            )
+        nc.sync.dma_start(facts[:], offs)
+        nc.sync.dma_start(atoms[:], offs2)
         for q in range(4):
             nc.sync.dma_start(
                 tab_s[32 * q : 32 * q + 4, :].bitcast(I32), tab_scales[0, 4 * q : 4 * q + 4, :].bitcast(I32)
             )
-        nc.sync.dma_start(atoms[:], offs2)
+
+        tab_w = ring.tile([P, T], U32, name="tab_w", tag="slot_a", align_bytes=64)
+        nc.sync.dma_start(tab_w[:].bitcast(I32), tab_words[0].rearrange("p t i -> p (t i)").bitcast(I32))
+
+        for q in range(4):
+            nc.sync.dma_start(
+                w1_s[32 * q : 32 * q + 4, :].bitcast(I32), w1_scales[0, 4 * q : 4 * q + 4, :].bitcast(I32)
+            )
 
         nc.vector.tensor_copy(
             w1p_w[:].bitcast(U16).rearrange("p (b i m) -> p b i m", b=PASSES, i=PACK),
             w1_w[:].rearrange("p (b m i) -> p b i m", b=PASSES, i=PACK),
         )
+        nc.vector.tensor_copy(v_s[:], tab_s[:].indirect(facts[:]))
         nc.vector.tensor_copy(
             w1p_s[:].rearrange("p (b i m) -> p b i m", b=PASSES, i=PACK),
             w1_s[:].rearrange("p (b m i) -> p b i m", b=PASSES, i=PACK),
         )
-        nc.vector.tensor_copy(v_s[:], tab_s[:].indirect(facts[:]))
-
-        tab_w = ring.tile([P, T], U32, name="tab_w", tag="slot_a", align_bytes=64)
-        nc.sync.dma_start(tab_w[:].bitcast(I32), tab_words[0].rearrange("p t i -> p (t i)").bitcast(I32))
 
         early = ring.tile([P, PLANES + (1 + EARLY) * M], F32, name="early", tag="slot_b", align_bytes=64)
         gain_sb = early[:, 0:PLANES]
@@ -123,9 +125,12 @@ def tile_list_soft_datalog_firing_kernel(
         nc.gpsimd.tensor_scalar(minus_wgt, minus_wgt, -1.0, 0.0, ALU.mult, ALU.add)
         prior_on_gpsimd(1, prior[1])
 
+        v_first = keep.tile([P, BANK], U32, name="v_first", align_bytes=64)
+        v_rest = ring.tile([P, (SLICES - 1) * BANK], U32, name="v_rest", tag="slot_d", align_bytes=64)
+        v_w = [v_first[:]] + [v_rest[:, s * BANK : (s + 1) * BANK] for s in range(SLICES - 1)]
         cols = BANK // 16
         for s in range(SLICES):
-            nc.vector.tensor_copy(v_w[s][:], tab_w[:].indirect(facts[:, s * cols : (s + 1) * cols]))
+            nc.vector.tensor_copy(v_w[s], tab_w[:].indirect(facts[:, s * cols : (s + 1) * cols]))
 
         res = ring.tile([P, N_TILES, M], F32, name="res", tag="slot_a", align_bytes=64)
 
@@ -142,7 +147,7 @@ def tile_list_soft_datalog_firing_kernel(
                 out=acc[:],
                 lhsT=w1p_w[:, 2 * P * q : 2 * P * (q + 1)].bitcast(FP4X4),
                 lhsT_scale=w1p_s[:, P * q : P * (q + 1)],
-                rhs=v_w[s][:].bitcast(FP8X4),
+                rhs=v_w[s].bitcast(FP8X4),
                 rhs_scale=v_s[:, s * BANK : (s + 1) * BANK],
                 start=True,
                 stop=True,
@@ -230,8 +235,14 @@ def tile_list_soft_datalog_firing_kernel(
 
         zs = {}
 
-        def new_z(b):
-            zs[b] = ring.tile([P, PACK * M], BF16, name="z", tag="pair%d" % b, align_bytes=64)
+        def new_z(b, j, chunks, tag):
+            tile = ring.tile([P, PACK * CHUNK * chunks], BF16, name="z", tag=tag, align_bytes=64)
+            for k in range(chunks):
+                zs[b, j + k] = (tile, j * CHUNK)
+
+        def z_cols(b, m0, width):
+            tile, first = zs[b, m0 // CHUNK]
+            return tile[:, PACK * (m0 - first) : PACK * (m0 - first + width)]
 
         def backward(b, j):
             back = bank("back")[:].rearrange("p (k u m) -> p k u m", u=2, m=P)
@@ -241,15 +252,13 @@ def tile_list_soft_datalog_firing_kernel(
                     words = rounded[2 * b + u][:].bitcast(F32)
                     nc.tensor.transpose(back[:, k, u, :], words[:, m0 : m0 + P], ident[:])
             nc.scalar.copy(
-                zs[b][:, PACK * j * CHUNK : PACK * (j + 1) * CHUNK]
-                .bitcast(F32)
-                .rearrange("p (k m u) -> p k m u", u=2, m=P),
+                z_cols(b, j * CHUNK, CHUNK).bitcast(F32).rearrange("p (k m u) -> p k m u", u=2, m=P),
                 back.rearrange("p k u m -> p k m u"),
             )
 
         def join_on_vector(m0, width):
             nc.vector.tensor_tensor(
-                zs[1][:, PACK * m0 : PACK * (m0 + width)].rearrange("p (c e i) -> p c i e", e=2, i=PACK),
+                z_cols(1, m0, width).rearrange("p (c e i) -> p c i e", e=2, i=PACK),
                 prior1[:, :, m0 : m0 + width].rearrange("p i (c e) -> p c i e", e=2),
                 picked1[:, :, m0 : m0 + width].rearrange("p i (c e) -> p c i e", e=2),
                 ALU.add,
@@ -260,13 +269,13 @@ def tile_list_soft_datalog_firing_kernel(
             nc.vector.quantize_mx(
                 out=z_w[:, b, cols].bitcast(FP8X4),
                 scales=z_s[:, b, cols],
-                in_=zs[b][:, PACK * m0 : PACK * (m0 + width)],
+                in_=z_cols(b, m0, width),
             )
 
         w2_bf = {}
 
         def round_w2(b):
-            w2_bf[b] = ring.tile([P, N * PACK], BF16, name="w2_bf", bufs=2, align_bytes=64)
+            w2_bf[b] = ring.tile([P, N * PACK], BF16, name="w2_bf", tag="w2_bf%d" % b, align_bytes=64)
             nc.scalar.copy(
                 w2_bf[b][:].rearrange("p (c e i) -> p c i e", e=2, i=PACK),
                 w2_raw[:, b].rearrange("p i (c e) -> p c i e", e=2),
@@ -347,50 +356,47 @@ def tile_list_soft_datalog_firing_kernel(
         slope(5)
         plane_with_forward(5, 0, 2)
         pick(4)
-        round_w2(0)
         slope(6)
         new_rounded(1)
         plane_with_forward(6, 1, 0)
         pick(5)
-        quantise_w2(0)
         slope(7)
         plane_with_forward(7, 1, 2)
         pick(6)
-        new_z(0)
-        new_z(1)
-        new_rounded(2)
-        new_rounded(3)
-        round_w2(1)
-        pick(7, 0, CHUNK)
-        pick(7, CHUNK, CHUNK)
-        backward(0, 1)
-        backward(0, 2)
-        forward(2, 0)
-        forward(3, 0)
-        join_on_vector(CHUNK, CHUNK)
-        quantise_w2(1)
-        quantise_z(0, CHUNK, CHUNK)
-        quantise_z(1, CHUNK, CHUNK)
-        pick(7, 2 * CHUNK, CHUNK)
-        both_products(CHUNK, CHUNK)
+        new_z(0, 0, CHUNKS, "pair0")
+        new_z(1, 0, 1, "pair1")
         backward(0, 0)
-        join_on_vector(2 * CHUNK, CHUNK)
-        quantise_z(0, 2 * CHUNK, CHUNK)
-        store(CHUNK, CHUNK, False)
-        backward(1, 0)
-        backward(0, 3)
-        quantise_z(1, 2 * CHUNK, CHUNK)
-        pick(7, 3 * CHUNK, CHUNK)
-        both_products(2 * CHUNK, CHUNK)
+        round_w2(0)
+        round_w2(1)
+        for j in range(1, CHUNKS):
+            backward(0, j)
+        pick(7, 0, CHUNK)
+        join_on_vector(0, CHUNK)
+        quantise_w2(0)
         quantise_z(0, 0, CHUNK)
+        pick(7, CHUNK, CHUNK)
+        quantise_w2(1)
         quantise_z(1, 0, CHUNK)
-        store(2 * CHUNK, CHUNK, False)
         both_products(0, CHUNK)
-        quantise_z(0, 3 * CHUNK, CHUNK)
+        new_z(1, 1, 1, "w2_bf1")
+        join_on_vector(CHUNK, CHUNK)
+        quantise_z(0, CHUNK, CHUNK)
+        quantise_z(0, 2 * CHUNK, 2 * CHUNK)
+        pick(7, 2 * CHUNK, CHUNK)
+        quantise_z(1, CHUNK, CHUNK)
+        store(0, CHUNK, False)
+        both_products(CHUNK, CHUNK)
+        new_z(1, 2, 1, "pair0")
+        join_on_vector(2 * CHUNK, CHUNK)
+        pick(7, 3 * CHUNK, CHUNK)
+        quantise_z(1, 2 * CHUNK, CHUNK)
+        store(CHUNK, CHUNK, False)
+        both_products(2 * CHUNK, CHUNK)
+        new_z(1, 3, 1, "w2_bf1")
         for h in range(2):
             join_on_vector(3 * CHUNK + h * P, P)
             second_product(0, 3 * CHUNK + h * P, P)
-        store(0, CHUNK, False)
+        store(2 * CHUNK, CHUNK, False)
         for h in range(2):
             quantise_z(1, 3 * CHUNK + h * P, P)
             second_product(1, 3 * CHUNK + h * P, P)

@@ -194,6 +194,19 @@ def tile_list_soft_datalog_firing_kernel(
                         ALU.mult,
                     )
 
+        last_slopes = {}
+
+        def last_slope(h, tag):
+            last_slopes[h] = ring.tile([P, BANK], F32, name="last_slope", tag=tag, align_bytes=64)
+            nc.vector.scalar_tensor_tensor(
+                last_slopes[h][:],
+                prior[PLANES - 1][:, h * BANK : (h + 1) * BANK],
+                gain_sb[:, PLANES - 1 : PLANES],
+                wgt_ps[h][:],
+                ALU.subtract,
+                ALU.mult,
+            )
+
         def late_prior(q):
             raw = ring.tile([P, M], F32, name="raw", tag=slope_tag(q - PACK))
             nc.sync.dma_start(raw[:], c_view[1, :, q - PACK, :])
@@ -208,6 +221,15 @@ def tile_list_soft_datalog_firing_kernel(
                 picked[q][:, m0 : m0 + width],
                 truth[q][:].indirect(atoms[:, m0 // 16 : (m0 + width) // 16]),
                 slopes[q][:, m0 : m0 + width],
+                ALU.mult,
+            )
+
+        def pick_last(j):
+            h, part = divmod(j, BANK // CHUNK)
+            nc.vector.tensor_tensor(
+                picked[PLANES - 1][:, j * CHUNK : (j + 1) * CHUNK],
+                truth[PLANES - 1][:].indirect(atoms[:, j * CHUNK // 16 : (j + 1) * CHUNK // 16]),
+                last_slopes[h][:, part * CHUNK : (part + 1) * CHUNK],
                 ALU.mult,
             )
 
@@ -286,42 +308,54 @@ def tile_list_soft_datalog_firing_kernel(
 
         out_view = out.rearrange("(t p) m -> p t m", p=P)
 
-        banks = {}
+        evidence = {}
+
+        def open_chunk(m0):
+            for u in range(2):
+                tile = bank("evidence")
+                for half in range(2):
+                    evidence[m0, 2 * u + half] = (tile[:, half * CHUNK : (half + 1) * CHUNK], half == 0, half == 1)
+
+        def open_piece(m0, h):
+            tiles = [psum.tile([P, BANK], F32, name="evidence", tag="wgt_ps%d" % h), bank("evidence")]
+            for t in range(N_TILES):
+                u, half = divmod(t, 2)
+                evidence[m0, t] = (tiles[u][:, half * P : (half + 1) * P], half == 0, half == 1)
 
         def second_product(b, m0, width):
             cols = slice(m0, m0 + width)
             for t in range(N_TILES):
-                u, half = divmod(t, 2)
-                if b == 0 and half == 0:
-                    banks[m0, u] = psum.tile([P, 2, width], F32, name="evidence", tag="acc", bufs=ACC_BANKS)
+                acc, opens, closes = evidence[m0, t]
                 nc.tensor.matmul_mx(
-                    out=banks[m0, u][:, half, :],
+                    out=acc,
                     lhsT=w2_w[:, b, t * P : (t + 1) * P].bitcast(FP8X4),
                     lhsT_scale=w2_s[:, b, t * P : (t + 1) * P],
                     rhs=z_w[:, b, cols].bitcast(FP8X4),
                     rhs_scale=z_s[:, b, cols],
-                    start=(b == 0 and half == 0),
-                    stop=(b == PASSES - 1 and half == 1),
+                    start=(b == 0 and opens),
+                    stop=(b == PASSES - 1 and closes),
                 )
 
-        def store(m0, width, shared):
-            cols = slice(m0, m0 + width)
+        def store_chunk(m0):
+            cols = slice(m0, m0 + CHUNK)
             for t in range(N_TILES):
-                u, half = divmod(t, 2)
-                if u == 0 or not shared:
+                nc.scalar.activation(res[:, t, cols], evidence[m0, t][0], ACT.Identity, bias=bias_sb[:, t : t + 1])
+                if t % 2 == 1:
+                    nc.sync.dma_start(out_view[:, t - 1 : t + 1, cols], res[:, t - 1 : t + 1, cols])
+
+        def store_piece(m0):
+            cols = slice(m0, m0 + P)
+            for t in range(N_TILES):
+                if t < 2:
                     nc.scalar.activation(
-                        res[:, t, cols], banks[m0, u][:, half, :], ACT.Identity, bias=bias_sb[:, t : t + 1]
+                        res[:, t, cols], evidence[m0, t][0], ACT.Identity, bias=bias_sb[:, t : t + 1]
                     )
                 else:
                     nc.vector.tensor_scalar(
-                        res[:, t, cols], banks[m0, u][:, half, :], bias_sb[:, t : t + 1], None, ALU.add
+                        res[:, t, cols], evidence[m0, t][0], bias_sb[:, t : t + 1], None, ALU.add
                     )
-                if half == 1:
+                if t % 2 == 1:
                     nc.sync.dma_start(out_view[:, t - 1 : t + 1, cols], res[:, t - 1 : t + 1, cols])
-
-        def both_products(m0, width):
-            second_product(0, m0, width)
-            second_product(1, m0, width)
 
         for s in range(SLICES):
             first_product(0, s)
@@ -360,44 +394,54 @@ def tile_list_soft_datalog_firing_kernel(
         new_rounded(1)
         plane_with_forward(6, 1, 0)
         pick(5)
-        slope(7)
+        last_slope(0, "slope_a")
         plane_with_forward(7, 1, 2)
         pick(6)
         new_z(0, 0, CHUNKS, "pair0")
         new_z(1, 0, 1, "pair1")
-        backward(0, 0)
+        new_z(1, 1, 1, "z_b")
         round_w2(0)
+        backward(0, 0)
         round_w2(1)
         for j in range(1, CHUNKS):
             backward(0, j)
-        pick(7, 0, CHUNK)
+        pick_last(0)
+        pick_last(1)
         join_on_vector(0, CHUNK)
+        join_on_vector(CHUNK, CHUNK)
         quantise_w2(0)
         quantise_z(0, 0, CHUNK)
-        pick(7, CHUNK, CHUNK)
+        open_chunk(0)
+        second_product(0, 0, CHUNK)
         quantise_w2(1)
         quantise_z(1, 0, CHUNK)
-        both_products(0, CHUNK)
-        new_z(1, 1, 1, "w2_bf1")
-        join_on_vector(CHUNK, CHUNK)
+        last_slope(1, "w2_bf1")
+        second_product(1, 0, CHUNK)
         quantise_z(0, CHUNK, CHUNK)
-        quantise_z(0, 2 * CHUNK, 2 * CHUNK)
-        pick(7, 2 * CHUNK, CHUNK)
         quantise_z(1, CHUNK, CHUNK)
-        store(0, CHUNK, False)
-        both_products(CHUNK, CHUNK)
+        open_chunk(CHUNK)
+        second_product(0, CHUNK, CHUNK)
+        second_product(1, CHUNK, CHUNK)
+        store_chunk(0)
+        pick_last(2)
+        quantise_z(0, 2 * CHUNK, 2 * CHUNK)
+        open_chunk(2 * CHUNK)
+        second_product(0, 2 * CHUNK, CHUNK)
+        for h in range(2):
+            open_piece(3 * CHUNK + h * P, h)
+            second_product(0, 3 * CHUNK + h * P, P)
         new_z(1, 2, 1, "pair0")
         join_on_vector(2 * CHUNK, CHUNK)
-        pick(7, 3 * CHUNK, CHUNK)
+        pick_last(3)
         quantise_z(1, 2 * CHUNK, CHUNK)
-        store(CHUNK, CHUNK, False)
-        both_products(2 * CHUNK, CHUNK)
-        new_z(1, 3, 1, "w2_bf1")
+        store_chunk(CHUNK)
+        second_product(1, 2 * CHUNK, CHUNK)
+        new_z(1, 3, 1, "z_b")
         for h in range(2):
             join_on_vector(3 * CHUNK + h * P, P)
-            second_product(0, 3 * CHUNK + h * P, P)
-        store(2 * CHUNK, CHUNK, False)
+        store_chunk(2 * CHUNK)
         for h in range(2):
             quantise_z(1, 3 * CHUNK + h * P, P)
             second_product(1, 3 * CHUNK + h * P, P)
-            store(3 * CHUNK + h * P, P, True)
+        for h in range(2):
+            store_piece(3 * CHUNK + h * P)

@@ -53,20 +53,18 @@ def tile_list_soft_datalog_firing_kernel(
         w2_s = keep.tile([P, PASSES, N], U8, name="w2_s", align_bytes=64)
         z_w = keep.tile([P, PASSES, M], U32, name="z_w", align_bytes=64)
         z_s = keep.tile([P, PASSES, M], U8, name="z_s", align_bytes=64)
-        warm = keep.tile([P, 2], F32, name="warm")
+        warm = keep.tile([P, 1], F32, name="warm")
         zeros = ring.tile([P, H // 4], I32, name="zeros", tag="slot_a", align_bytes=64)
 
-        nc.vector.memset(warm[:, 0:1], 0.0)
         nc.vector.memset(tab_s[:].bitcast(I32), 0)
         nc.vector.memset(zeros[:], 0)
         nc.vector.tensor_copy(w1_s[:].bitcast(I32), zeros[:])
-        nc.scalar.activation(warm[:, 1:2], warm[:, 0:1], ACT.Sigmoid)
-
         make_identity(nc, ident[:])
+        nc.scalar.activation(warm[:], ident[:, 0:1], ACT.Sigmoid)
 
-        nc.sync.dma_start(w1_w[:].bitcast(I32), w1_words[0].bitcast(I32))
         nc.sync.dma_start(facts[:], offs)
         nc.sync.dma_start(atoms[:], offs2)
+        nc.sync.dma_start(w1_w[:].bitcast(I32), w1_words[0].bitcast(I32))
         for q in range(4):
             nc.sync.dma_start(
                 tab_s[32 * q : 32 * q + 4, :].bitcast(I32), tab_scales[0, 4 * q : 4 * q + 4, :].bitcast(I32)
@@ -74,7 +72,6 @@ def tile_list_soft_datalog_firing_kernel(
 
         tab_w = ring.tile([P, T], U32, name="tab_w", tag="slot_a", align_bytes=64)
         nc.sync.dma_start(tab_w[:].bitcast(I32), tab_words[0].rearrange("p t i -> p (t i)").bitcast(I32))
-
         for q in range(4):
             nc.sync.dma_start(
                 w1_s[32 * q : 32 * q + 4, :].bitcast(I32), w1_scales[0, 4 * q : 4 * q + 4, :].bitcast(I32)
@@ -90,40 +87,60 @@ def tile_list_soft_datalog_firing_kernel(
             w1_s[:].rearrange("p (b m i) -> p b i m", b=PASSES, i=PACK),
         )
 
-        early = ring.tile([P, PLANES + (1 + EARLY) * M], F32, name="early", tag="slot_b", align_bytes=64)
+        early = ring.tile([P, PLANES + (EARLY + 1) * M], F32, name="early", tag="slot_b", align_bytes=64)
         gain_sb = early[:, 0:PLANES]
-        minus_wgt = early[:, PLANES : PLANES + M]
         c_view = c.rearrange("(b p i) m -> b p i m", p=P, i=PACK)
         w2_view = w2.rearrange("(b p i) n -> b p i n", p=P, i=PACK)
-        prior = [early[:, PLANES + (1 + q) * M : PLANES + (2 + q) * M] for q in range(EARLY)]
+        prior = [early[:, PLANES + q * M : PLANES + (1 + q) * M] for q in range(EARLY)]
 
+        wgt_sb = early[:, PLANES + EARLY * M :]
+        nc.sync.dma_start(wgt_sb, wgt)
         nc.sync.dma_start(
             gain_sb.rearrange("p (b i) -> p b i", i=PACK), gain.rearrange("(b p i) -> p b i", p=P, i=PACK)
         )
-        nc.sync.dma_start(prior[0], c_view[0, :, 0, :])
-        nc.sync.dma_start(minus_wgt, wgt)
-        for q in range(1, EARLY):
+        for q in range(EARLY):
             nc.sync.dma_start(prior[q], c_view[0, :, q, :])
 
-        late = ring.tile([P, 2 * M + PLANES * N + N_TILES], F32, name="late", tag="slot_c", align_bytes=64)
-        prior.extend([late[:, q * M : (q + 1) * M] for q in range(2)])
-        w2_raw = late[:, 2 * M : 2 * M + PLANES * N].rearrange("p (b i n) -> p b i n", b=PASSES, i=PACK)
-        bias_sb = late[:, 2 * M + PLANES * N :]
-        for q in range(EARLY, PACK):
-            nc.sync.dma_start(prior[q], c_view[0, :, q, :])
+        rest = PLANES - EARLY
+        late = ring.tile([P, rest * M + PLANES * N + N_TILES], F32, name="late", tag="slot_c", align_bytes=64)
+        prior.extend([late[:, q * M : (q + 1) * M] for q in range(rest)])
+        prior1 = late[:, (PACK - EARLY) * M : rest * M].rearrange("p (i m) -> p i m", i=PACK)
+        w2_raw = late[:, rest * M : rest * M + PLANES * N].rearrange("p (b i n) -> p b i n", b=PASSES, i=PACK)
+        bias_sb = late[:, rest * M + PLANES * N :]
+        for q in range(EARLY, PLANES):
+            nc.sync.dma_start(prior[q], c_view[q // PACK, :, q % PACK, :])
         for b in range(PASSES):
             nc.sync.dma_start(w2_raw[:, b], w2_view[b])
         with nc.allow_non_contiguous_dma(reason="one bias value a partition"):
             nc.sync.dma_start(bias_sb, bias.rearrange("(t p) -> p t", p=P))
-        prior1 = keep.tile([P, PACK, M], F32, name="prior1")
-        prior.extend([prior1[:, i, :] for i in range(PACK)])
 
-        def prior_on_gpsimd(q, raw):
-            nc.gpsimd.tensor_scalar(prior[q], raw, gain_sb[:, q : q + 1], 0.0, ALU.mult, ALU.add)
+        wgt_ps = [psum.tile([P, BANK], F32, name="wgt_ps", tag="wgt_ps%d" % h) for h in range(M // BANK)]
 
-        prior_on_gpsimd(0, prior[0])
-        nc.gpsimd.tensor_scalar(minus_wgt, minus_wgt, -1.0, 0.0, ALU.mult, ALU.add)
-        prior_on_gpsimd(1, prior[1])
+        def bank(name):
+            return psum.tile([P, BANK], F32, name=name, tag="acc", bufs=ACC_BANKS)
+
+        across = {}
+
+        def wgt_forward(h):
+            turned = bank("wgt_turned")
+            for k in range(PACK):
+                m0 = h * BANK + k * P
+                nc.tensor.transpose(turned[:, k * P : (k + 1) * P], wgt_sb[:, m0 : m0 + P], ident[:])
+            across[h] = ring.tile([P, BANK], F32, name="across", tag="rounded%d" % h)
+            nc.scalar.activation(across[h][:], turned[:], ACT.Copy, scale=-1.0)
+
+        def wgt_backward(h):
+            for k in range(PACK):
+                nc.tensor.transpose(wgt_ps[h][:, k * P : (k + 1) * P], across[h][:, k * P : (k + 1) * P], ident[:])
+
+        def prior_on_scalar(q):
+            nc.scalar.activation(prior[q], prior[q], ACT.Copy, scale=gain_sb[:, q : q + 1])
+
+        def priors_on_gpsimd(planes, tag):
+            zero = ring.tile([P, 1], F32, name="zero", tag=tag, align_bytes=64)
+            nc.gpsimd.memset(zero[:], 0.0)
+            for q in planes:
+                nc.gpsimd.tensor_scalar(prior[q], prior[q], gain_sb[:, q : q + 1], zero[:], ALU.mult, ALU.add)
 
         v_first = keep.tile([P, BANK], U32, name="v_first", align_bytes=64)
         v_rest = ring.tile([P, (SLICES - 1) * BANK], U32, name="v_rest", tag="slot_d", align_bytes=64)
@@ -132,16 +149,14 @@ def tile_list_soft_datalog_firing_kernel(
         for s in range(SLICES):
             nc.vector.tensor_copy(v_w[s], tab_w[:].indirect(facts[:, s * cols : (s + 1) * cols]))
 
+        priors_on_gpsimd((2, 3), "slot_a")
         res = ring.tile([P, N_TILES, M], F32, name="res", tag="slot_a", align_bytes=64)
 
         truth = {}
 
-        def bank(name):
-            return psum.tile([P, BANK], F32, name=name, tag="acc", bufs=ACC_BANKS)
-
         def first_product(q, s):
             if s == 0:
-                truth[q] = ring.tile([P, S], F32, name="truth", tag="window%d" % q)
+                truth[q] = ring.tile([P, S], F32, name="truth", tag="window%d" % q, align_bytes=64)
             acc = bank("acc")
             nc.tensor.matmul_mx(
                 out=acc[:],
@@ -158,41 +173,18 @@ def tile_list_soft_datalog_firing_kernel(
             for s in range(SLICES):
                 first_product(q, s)
 
-        wgt_ps = [psum.tile([P, BANK], F32, name="wgt_ps", tag="wgt_ps%d" % h) for h in range(M // BANK)]
-
-        def wgt_to_psum():
-            for h in range(M // BANK):
-                turned = bank("wgt_turned")
-                for k in range(PACK):
-                    m0 = h * BANK + k * P
-                    nc.tensor.transpose(turned[:, k * P : (k + 1) * P], minus_wgt[:, m0 : m0 + P], ident[:])
-                across = ring.tile([P, BANK], F32, name="across", tag="rounded%d" % h)
-                nc.scalar.copy(across[:], turned[:])
-                for k in range(PACK):
-                    nc.tensor.transpose(wgt_ps[h][:, k * P : (k + 1) * P], across[:, k * P : (k + 1) * P], ident[:])
-
         slopes = {}
 
         def slope_tag(q):
-            return "slope%d" % q if q < EARLY else "window%d" % (q - 2)
+            return ("slope0", "slope1", "window0", "window1", "slope1", "slope5", "slope6")[q]
 
         def slope(q):
-            slopes[q] = ring.tile([P, M], F32, name="slope", tag=slope_tag(q))
-            if q < EARLY:
+            slopes[q] = ring.tile([P, M], F32, name="slope", tag=slope_tag(q), align_bytes=64)
+            for h in range(M // BANK):
+                half = slice(h * BANK, (h + 1) * BANK)
                 nc.vector.scalar_tensor_tensor(
-                    slopes[q][:], prior[q], gain_sb[:, q : q + 1], minus_wgt, ALU.subtract, ALU.mult
+                    slopes[q][:, half], prior[q][:, half], gain_sb[:, q : q + 1], wgt_ps[h][:], ALU.subtract, ALU.mult
                 )
-            else:
-                for h in range(M // BANK):
-                    half = slice(h * BANK, (h + 1) * BANK)
-                    nc.vector.scalar_tensor_tensor(
-                        slopes[q][:, half],
-                        prior[q][:, half],
-                        gain_sb[:, q : q + 1],
-                        wgt_ps[h][:],
-                        ALU.subtract,
-                        ALU.mult,
-                    )
 
         last_slopes = {}
 
@@ -206,11 +198,6 @@ def tile_list_soft_datalog_firing_kernel(
                 ALU.subtract,
                 ALU.mult,
             )
-
-        def late_prior(q):
-            raw = ring.tile([P, M], F32, name="raw", tag=slope_tag(q - PACK))
-            nc.sync.dma_start(raw[:], c_view[1, :, q - PACK, :])
-            prior_on_gpsimd(q, raw[:])
 
         pairs0 = [ring.tile([P, 2, M], F32, name="picked0", tag="pair%d" % u, align_bytes=64) for u in range(2)]
         picked1 = keep.tile([P, PACK, M], F32, name="picked1")
@@ -357,25 +344,27 @@ def tile_list_soft_datalog_firing_kernel(
                 if t % 2 == 1:
                     nc.sync.dma_start(out_view[:, t - 1 : t + 1, cols], res[:, t - 1 : t + 1, cols])
 
-        for s in range(SLICES):
+        wgt_forward(0)
+        wgt_forward(1)
+        prior_on_scalar(0)
+        first_product(0, 0)
+        wgt_backward(0)
+        wgt_backward(1)
+        prior_on_scalar(1)
+        for s in range(1, SLICES):
             first_product(0, s)
-            first_product(1, s)
-            if s in (1, 3):
-                slope(s // 2)
-        nc.scalar.activation(prior[2], prior[2], ACT.Copy, scale=gain_sb[:, 2:3])
-        wgt_to_psum()
+        slope(0)
+        slope(1)
+        truth_plane(1)
         pick(0)
-        prior_on_gpsimd(3, prior[3])
-        late_prior(4)
-        slope(2)
+        priors_on_gpsimd((4, 5, 6, 7), slope_tag(0))
         truth_plane(2)
         pick(1)
-        late_prior(5)
-        slope(3)
+        for q in range(2, PLANES - 1):
+            slope(q)
+        last_slope(0, "slope_a")
         truth_plane(3)
         pick(2)
-        late_prior(6)
-        slope(4)
 
         def plane_with_forward(q, g, j):
             for half in range(2):
@@ -386,17 +375,15 @@ def tile_list_soft_datalog_firing_kernel(
         new_rounded(0)
         plane_with_forward(4, 0, 0)
         pick(3)
-        late_prior(7)
-        slope(5)
         plane_with_forward(5, 0, 2)
         pick(4)
-        slope(6)
-        new_rounded(1)
-        plane_with_forward(6, 1, 0)
+        truth_plane(6)
         pick(5)
-        last_slope(0, "slope_a")
-        plane_with_forward(7, 1, 2)
+        new_rounded(1)
+        plane_with_forward(7, 1, 0)
         pick(6)
+        forward(1, 2)
+        forward(1, 3)
         new_z(0, 0, CHUNKS, "pair0")
         new_z(1, 0, 1, "pair1")
         new_z(1, 1, 1, "z_b")

@@ -133,8 +133,8 @@ def tile_list_soft_datalog_firing_kernel(
             for k in range(PACK):
                 nc.tensor.transpose(wgt_ps[h][:, k * P : (k + 1) * P], across[h][:, k * P : (k + 1) * P], ident[:])
 
-        def prior_on_scalar(q):
-            nc.scalar.activation(prior[q], prior[q], ACT.Copy, scale=gain_sb[:, q : q + 1])
+        for q in range(PACK):
+            nc.gpsimd.tensor_scalar(prior[q], prior[q], gain_sb[:, q : q + 1], 0.0, ALU.mult, ALU.add)
 
         def priors_on_gpsimd(planes, tag):
             zero = ring.tile([P, 1], F32, name="zero", tag=tag, align_bytes=64)
@@ -149,7 +149,6 @@ def tile_list_soft_datalog_firing_kernel(
         for s in range(SLICES):
             nc.vector.tensor_copy(v_w[s], tab_w[:].indirect(facts[:, s * cols : (s + 1) * cols]))
 
-        priors_on_gpsimd((2, 3), "slot_a")
         res = ring.tile([P, N_TILES, M], F32, name="res", tag="slot_a", align_bytes=64)
 
         truth = {}
@@ -346,11 +345,9 @@ def tile_list_soft_datalog_firing_kernel(
 
         wgt_forward(0)
         wgt_forward(1)
-        prior_on_scalar(0)
         first_product(0, 0)
         wgt_backward(0)
         wgt_backward(1)
-        prior_on_scalar(1)
         for s in range(1, SLICES):
             first_product(0, s)
         slope(0)
@@ -385,7 +382,7 @@ def tile_list_soft_datalog_firing_kernel(
         forward(1, 2)
         forward(1, 3)
         new_z(0, 0, CHUNKS, "pair0")
-        new_z(1, 0, 1, "pair1")
+        new_z(1, 0, 1, "z_a")
         new_z(1, 1, 1, "z_b")
         round_w2(0)
         backward(0, 0)

@@ -48,27 +48,29 @@ def tile_list_soft_datalog_firing_kernel(
         w1p_w = keep.tile([P, 2 * H], U8, name="w1p_w", align_bytes=64)
         w1p_s = keep.tile([P, H], U8, name="w1p_s", align_bytes=64)
         v_s = keep.tile([P, S], U8, name="v_s", align_bytes=64)
+        spread_s = keep.tile([P, S], U8, name="spread_s", align_bytes=64)
         ident = keep.tile([P, P], F32, name="ident")
         w2_w = keep.tile([P, PASSES, N], U32, name="w2_w", align_bytes=64)
         w2_s = keep.tile([P, PASSES, N], U8, name="w2_s", align_bytes=64)
         z_w = keep.tile([P, PASSES, M], U32, name="z_w", align_bytes=64)
         z_s = keep.tile([P, PASSES, M], U8, name="z_s", align_bytes=64)
         warm = keep.tile([P, 1], F32, name="warm")
-        zeros = ring.tile([P, H // 4], I32, name="zeros", tag="slot_a", align_bytes=64)
+        zeros = [ring.tile([P, H // 8], I32, name="zeros", tag=tag, align_bytes=64) for tag in ("slot_a", "slot_w")]
 
-        nc.vector.memset(tab_s[:].bitcast(I32), 0)
-        nc.vector.memset(zeros[:], 0)
-        nc.vector.tensor_copy(w1_s[:].bitcast(I32), zeros[:])
+        for u in range(2):
+            nc.gpsimd.memset(zeros[u][:], 0)
+        nc.gpsimd.memset(tab_s[:, : T // 2].bitcast(I32), 0)
+        nc.vector.memset(tab_s[:, T // 2 :].bitcast(I32), 0)
+        for u in range(2):
+            nc.vector.tensor_copy(w1_s[:, u * H // 2 : (u + 1) * H // 2].bitcast(I32), zeros[u][:])
         make_identity(nc, ident[:])
+        nc.gpsimd.memset(v_s[:].bitcast(I32), 0)
         nc.scalar.activation(warm[:], ident[:, 0:1], ACT.Sigmoid)
 
+        nc.sync.dma_start(w1_w[:].bitcast(I32), w1_words[0].bitcast(I32))
         nc.sync.dma_start(facts[:], offs)
         nc.sync.dma_start(atoms[:], offs2)
-        nc.sync.dma_start(w1_w[:].bitcast(I32), w1_words[0].bitcast(I32))
-        for q in range(4):
-            nc.sync.dma_start(
-                tab_s[32 * q : 32 * q + 4, :].bitcast(I32), tab_scales[0, 4 * q : 4 * q + 4, :].bitcast(I32)
-            )
+        nc.sync.dma_start(tab_s[0:P:8, :].bitcast(I32), tab_scales[0].bitcast(I32))
 
         tab_w = ring.tile([P, T], U32, name="tab_w", tag="slot_a", align_bytes=64)
         nc.sync.dma_start(tab_w[:].bitcast(I32), tab_words[0].rearrange("p t i -> p (t i)").bitcast(I32))
@@ -81,33 +83,32 @@ def tile_list_soft_datalog_firing_kernel(
             w1p_w[:].bitcast(U16).rearrange("p (b i m) -> p b i m", b=PASSES, i=PACK),
             w1_w[:].rearrange("p (b m i) -> p b i m", b=PASSES, i=PACK),
         )
-        nc.vector.tensor_copy(v_s[:], tab_s[:].indirect(facts[:]))
+        nc.vector.tensor_copy(spread_s[:], tab_s[:].indirect(facts[:]))
         nc.vector.tensor_copy(
             w1p_s[:].rearrange("p (b i m) -> p b i m", b=PASSES, i=PACK),
             w1_s[:].rearrange("p (b m i) -> p b i m", b=PASSES, i=PACK),
         )
 
-        early = ring.tile([P, PLANES + (EARLY + 1) * M], F32, name="early", tag="slot_b", align_bytes=64)
+        early = ring.tile([P, PLANES + M], F32, name="early", tag="slot_w", align_bytes=64)
         gain_sb = early[:, 0:PLANES]
         c_view = c.rearrange("(b p i) m -> b p i m", p=P, i=PACK)
         w2_view = w2.rearrange("(b p i) n -> b p i n", p=P, i=PACK)
-        prior = [early[:, PLANES + q * M : PLANES + (1 + q) * M] for q in range(EARLY)]
 
-        wgt_sb = early[:, PLANES + EARLY * M :]
+        wgt_sb = early[:, PLANES:]
         nc.sync.dma_start(wgt_sb, wgt)
         nc.sync.dma_start(
             gain_sb.rearrange("p (b i) -> p b i", i=PACK), gain.rearrange("(b p i) -> p b i", p=P, i=PACK)
         )
-        for q in range(EARLY):
-            nc.sync.dma_start(prior[q], c_view[0, :, q, :])
+        for r in range(4):
+            nc.sync.dma_start(v_s[r:P:32, :].bitcast(I32), spread_s[8 * r : P : 32, :].bitcast(I32))
 
-        rest = PLANES - EARLY
+        rest = PLANES
         late = ring.tile([P, rest * M + PLANES * N + N_TILES], F32, name="late", tag="slot_c", align_bytes=64)
-        prior.extend([late[:, q * M : (q + 1) * M] for q in range(rest)])
-        prior1 = late[:, (PACK - EARLY) * M : rest * M].rearrange("p (i m) -> p i m", i=PACK)
+        prior = [late[:, q * M : (q + 1) * M] for q in range(rest)]
+        prior1 = late[:, PACK * M : rest * M].rearrange("p (i m) -> p i m", i=PACK)
         w2_raw = late[:, rest * M : rest * M + PLANES * N].rearrange("p (b i n) -> p b i n", b=PASSES, i=PACK)
         bias_sb = late[:, rest * M + PLANES * N :]
-        for q in range(EARLY, PLANES):
+        for q in range(PLANES):
             nc.sync.dma_start(prior[q], c_view[q // PACK, :, q % PACK, :])
         for b in range(PASSES):
             nc.sync.dma_start(w2_raw[:, b], w2_view[b])
@@ -116,13 +117,16 @@ def tile_list_soft_datalog_firing_kernel(
 
         wgt_ps = [psum.tile([P, BANK], F32, name="wgt_ps", tag="wgt_ps%d" % h) for h in range(M // BANK)]
 
+        turns = []
+
         def bank(name):
-            return psum.tile([P, BANK], F32, name=name, tag="acc", bufs=ACC_BANKS)
+            turns.append(name)
+            return psum.tile([P, BANK], F32, name=name, tag="acc%d" % (len(turns) % ACC_BANKS))
 
         across = {}
 
         def wgt_forward(h):
-            turned = bank("wgt_turned")
+            turned = psum.tile([P, BANK], F32, name="wgt_turned", tag="acc%d" % (h + 1))
             for k in range(PACK):
                 m0 = h * BANK + k * P
                 nc.tensor.transpose(turned[:, k * P : (k + 1) * P], wgt_sb[:, m0 : m0 + P], ident[:])

@@ -367,24 +367,20 @@ def tile_list_soft_datalog_firing_kernel(
         truth_plane(3)
         pick(2)
 
-        def plane_with_forward(q, g, j):
-            for half in range(2):
-                forward(g, j + half)
-                first_product(q, 2 * half)
-                first_product(q, 2 * half + 1)
+        def plane_with_forward(q, j):
+            first_product(q, 0)
+            first_product(q, 1)
+            forward(0, j)
+            first_product(q, 2)
+            first_product(q, 3)
 
         new_rounded(0)
-        plane_with_forward(4, 0, 0)
-        pick(3)
-        plane_with_forward(5, 0, 2)
-        pick(4)
-        truth_plane(6)
-        pick(5)
+        for j in range(CHUNKS):
+            plane_with_forward(PACK + j, j)
+            pick(PACK - 1 + j)
         new_rounded(1)
-        plane_with_forward(7, 1, 0)
-        pick(6)
-        forward(1, 2)
-        forward(1, 3)
+        for j in range(CHUNKS):
+            forward(1, j)
         new_z(0, 0, CHUNKS, "pair0")
         new_z(1, 0, 1, "z_a")
         new_z(1, 1, 1, "z_b")

@@ -27,7 +27,6 @@ N_TILES = N // P
 CHUNK = 256
 CHUNKS = M // CHUNK
 ACC_BANKS = 6
-EARLY = 2
 
 
 def tile_list_soft_datalog_firing_kernel(
@@ -48,7 +47,7 @@ def tile_list_soft_datalog_firing_kernel(
         w1p_w = keep.tile([P, 2 * H], U8, name="w1p_w", align_bytes=64)
         w1p_s = keep.tile([P, H], U8, name="w1p_s", align_bytes=64)
         v_s = keep.tile([P, S], U8, name="v_s", align_bytes=64)
-        spread_s = keep.tile([P, S], U8, name="spread_s", align_bytes=64)
+        spread_s = ring.tile([P, S], U8, name="spread_s", tag="slot_s", align_bytes=64)
         ident = keep.tile([P, P], F32, name="ident")
         w2_w = keep.tile([P, PASSES, N], U32, name="w2_w", align_bytes=64)
         w2_s = keep.tile([P, PASSES, N], U8, name="w2_s", align_bytes=64)
@@ -57,9 +56,9 @@ def tile_list_soft_datalog_firing_kernel(
         warm = keep.tile([P, 1], F32, name="warm")
         zeros = [ring.tile([P, H // 8], I32, name="zeros", tag=tag, align_bytes=64) for tag in ("slot_a", "slot_w")]
 
+        nc.gpsimd.memset(tab_s[:, : T // 2].bitcast(I32), 0)
         for u in range(2):
             nc.gpsimd.memset(zeros[u][:], 0)
-        nc.gpsimd.memset(tab_s[:, : T // 2].bitcast(I32), 0)
         nc.vector.memset(tab_s[:, T // 2 :].bitcast(I32), 0)
         for u in range(2):
             nc.vector.tensor_copy(w1_s[:, u * H // 2 : (u + 1) * H // 2].bitcast(I32), zeros[u][:])
@@ -74,9 +73,10 @@ def tile_list_soft_datalog_firing_kernel(
 
         tab_w = ring.tile([P, T], U32, name="tab_w", tag="slot_a", align_bytes=64)
         nc.sync.dma_start(tab_w[:].bitcast(I32), tab_words[0].rearrange("p t i -> p (t i)").bitcast(I32))
-        for q in range(4):
+        for quad in range(4):
             nc.sync.dma_start(
-                w1_s[32 * q : 32 * q + 4, :].bitcast(I32), w1_scales[0, 4 * q : 4 * q + 4, :].bitcast(I32)
+                w1_s[32 * quad : 32 * quad + 4, :].bitcast(I32),
+                w1_scales[0, 4 * quad : 4 * quad + 4, :].bitcast(I32),
             )
 
         nc.vector.tensor_copy(
@@ -99,21 +99,21 @@ def tile_list_soft_datalog_firing_kernel(
         nc.sync.dma_start(
             gain_sb.rearrange("p (b i) -> p b i", i=PACK), gain.rearrange("(b p i) -> p b i", p=P, i=PACK)
         )
-        for r in range(4):
-            nc.sync.dma_start(v_s[r:P:32, :].bitcast(I32), spread_s[8 * r : P : 32, :].bitcast(I32))
+        for row in range(4):
+            nc.sync.dma_start(v_s[row:P:32, :].bitcast(I32), spread_s[8 * row : P : 32, :].bitcast(I32))
 
-        rest = PLANES
-        late = ring.tile([P, rest * M + PLANES * N + N_TILES], F32, name="late", tag="slot_c", align_bytes=64)
-        prior = [late[:, q * M : (q + 1) * M] for q in range(rest)]
-        prior1 = late[:, PACK * M : rest * M].rearrange("p (i m) -> p i m", i=PACK)
-        w2_raw = late[:, rest * M : rest * M + PLANES * N].rearrange("p (b i n) -> p b i n", b=PASSES, i=PACK)
-        bias_sb = late[:, rest * M + PLANES * N :]
+        late = ring.tile([P, PLANES * M + PACK * N + N_TILES], F32, name="late", tag="slot_c", align_bytes=64)
+        prior = [late[:, q * M : (q + 1) * M] for q in range(PLANES)]
+        prior1 = late[:, PACK * M : PLANES * M].rearrange("p (i m) -> p i m", i=PACK)
+        w2_last = ring.tile([P, PACK, N], F32, name="w2_last", tag="slot_s", align_bytes=64)
+        w2_raw = [late[:, PLANES * M : PLANES * M + PACK * N].rearrange("p (i n) -> p i n", i=PACK), w2_last[:]]
+        bias_sb = late[:, PLANES * M + PACK * N :]
         for q in range(PLANES):
             nc.sync.dma_start(prior[q], c_view[q // PACK, :, q % PACK, :])
-        for b in range(PASSES):
-            nc.sync.dma_start(w2_raw[:, b], w2_view[b])
         with nc.allow_non_contiguous_dma(reason="one bias value a partition"):
             nc.sync.dma_start(bias_sb, bias.rearrange("(t p) -> p t", p=P))
+        for b in range(PASSES):
+            nc.sync.dma_start(w2_raw[b], w2_view[b])
 
         wgt_ps = [psum.tile([P, BANK], F32, name="wgt_ps", tag="wgt_ps%d" % h) for h in range(M // BANK)]
 
@@ -140,18 +140,17 @@ def tile_list_soft_datalog_firing_kernel(
         for q in range(PACK):
             nc.gpsimd.tensor_scalar(prior[q], prior[q], gain_sb[:, q : q + 1], 0.0, ALU.mult, ALU.add)
 
-        def priors_on_gpsimd(planes, tag):
-            zero = ring.tile([P, 1], F32, name="zero", tag=tag, align_bytes=64)
+        def priors_of_pass_1():
+            zero = ring.tile([P, 1], F32, name="zero", tag="slope0", align_bytes=64)
             nc.gpsimd.memset(zero[:], 0.0)
-            for q in planes:
+            for q in range(PACK, PLANES):
                 nc.gpsimd.tensor_scalar(prior[q], prior[q], gain_sb[:, q : q + 1], zero[:], ALU.mult, ALU.add)
 
         v_first = keep.tile([P, BANK], U32, name="v_first", align_bytes=64)
         v_rest = ring.tile([P, (SLICES - 1) * BANK], U32, name="v_rest", tag="slot_d", align_bytes=64)
         v_w = [v_first[:]] + [v_rest[:, s * BANK : (s + 1) * BANK] for s in range(SLICES - 1)]
-        cols = BANK // 16
         for s in range(SLICES):
-            nc.vector.tensor_copy(v_w[s], tab_w[:].indirect(facts[:, s * cols : (s + 1) * cols]))
+            nc.vector.tensor_copy(v_w[s], tab_w[:].indirect(facts[:, s * BANK // 16 : (s + 1) * BANK // 16]))
 
         res = ring.tile([P, N_TILES, M], F32, name="res", tag="slot_a", align_bytes=64)
 
@@ -178,11 +177,10 @@ def tile_list_soft_datalog_firing_kernel(
 
         slopes = {}
 
-        def slope_tag(q):
-            return ("slope0", "slope1", "window0", "window1", "slope1", "slope5", "slope6")[q]
+        reused = {2: "window0", 3: "window1", 4: "slope1"}
 
         def slope(q):
-            slopes[q] = ring.tile([P, M], F32, name="slope", tag=slope_tag(q), align_bytes=64)
+            slopes[q] = ring.tile([P, M], F32, name="slope", tag=reused.get(q, "slope%d" % q), align_bytes=64)
             for h in range(M // BANK):
                 half = slice(h * BANK, (h + 1) * BANK)
                 nc.vector.scalar_tensor_tensor(
@@ -206,13 +204,8 @@ def tile_list_soft_datalog_firing_kernel(
         picked1 = keep.tile([P, PACK, M], F32, name="picked1")
         picked = [pairs0[q // 2][:, q % 2, :] for q in range(PACK)] + [picked1[:, i, :] for i in range(PACK)]
 
-        def pick(q, m0=0, width=M):
-            nc.vector.tensor_tensor(
-                picked[q][:, m0 : m0 + width],
-                truth[q][:].indirect(atoms[:, m0 // 16 : (m0 + width) // 16]),
-                slopes[q][:, m0 : m0 + width],
-                ALU.mult,
-            )
+        def pick(q):
+            nc.vector.tensor_tensor(picked[q], truth[q][:].indirect(atoms[:]), slopes[q][:], ALU.mult)
 
         def pick_last(j):
             h, part = divmod(j, BANK // CHUNK)
@@ -226,7 +219,7 @@ def tile_list_soft_datalog_firing_kernel(
         rounded = {}
 
         def new_rounded(g):
-            rounded[g] = ring.tile([P, 2 * M if g < 2 else M], BF16, name="rounded", tag="rounded%d" % g)
+            rounded[g] = ring.tile([P, 2 * M], BF16, name="rounded", tag="rounded%d" % g)
 
         def forward(g, j):
             turned = bank("turned")
@@ -256,15 +249,15 @@ def tile_list_soft_datalog_firing_kernel(
             tile, first = zs[b, m0 // CHUNK]
             return tile[:, PACK * (m0 - first) : PACK * (m0 - first + width)]
 
-        def backward(b, j):
+        def backward(j):
             back = bank("back")[:].rearrange("p (k u m) -> p k u m", u=2, m=P)
             for k in range(CHUNK // P):
                 m0 = j * CHUNK + k * P
                 for u in range(2):
-                    words = rounded[2 * b + u][:].bitcast(F32)
+                    words = rounded[u][:].bitcast(F32)
                     nc.tensor.transpose(back[:, k, u, :], words[:, m0 : m0 + P], ident[:])
             nc.scalar.copy(
-                z_cols(b, j * CHUNK, CHUNK).bitcast(F32).rearrange("p (k m u) -> p k m u", u=2, m=P),
+                z_cols(0, j * CHUNK, CHUNK).bitcast(F32).rearrange("p (k m u) -> p k m u", u=2, m=P),
                 back.rearrange("p k u m -> p k m u"),
             )
 
@@ -290,7 +283,7 @@ def tile_list_soft_datalog_firing_kernel(
             w2_bf[b] = ring.tile([P, N * PACK], BF16, name="w2_bf", tag="w2_bf%d" % b, align_bytes=64)
             nc.scalar.copy(
                 w2_bf[b][:].rearrange("p (c e i) -> p c i e", e=2, i=PACK),
-                w2_raw[:, b].rearrange("p i (c e) -> p c i e", e=2),
+                w2_raw[b].rearrange("p i (c e) -> p c i e", e=2),
             )
 
         def quantise_w2(b):
@@ -336,7 +329,7 @@ def tile_list_soft_datalog_firing_kernel(
         def store_piece(m0):
             cols = slice(m0, m0 + P)
             for t in range(N_TILES):
-                if t < 2:
+                if t < N_TILES // 2:
                     nc.scalar.activation(
                         res[:, t, cols], evidence[m0, t][0], ACT.Identity, bias=bias_sb[:, t : t + 1]
                     )
@@ -358,7 +351,7 @@ def tile_list_soft_datalog_firing_kernel(
         slope(1)
         truth_plane(1)
         pick(0)
-        priors_on_gpsimd((4, 5, 6, 7), slope_tag(0))
+        priors_of_pass_1()
         truth_plane(2)
         pick(1)
         for q in range(2, PLANES - 1):
@@ -381,14 +374,15 @@ def tile_list_soft_datalog_firing_kernel(
         new_rounded(1)
         for j in range(CHUNKS):
             forward(1, j)
+
         new_z(0, 0, CHUNKS, "pair0")
         new_z(1, 0, 1, "z_a")
         new_z(1, 1, 1, "z_b")
         round_w2(0)
-        backward(0, 0)
+        backward(0)
         round_w2(1)
         for j in range(1, CHUNKS):
-            backward(0, j)
+            backward(j)
         pick_last(0)
         pick_last(1)
         join_on_vector(0, CHUNK)
@@ -399,7 +393,7 @@ def tile_list_soft_datalog_firing_kernel(
         second_product(0, 0, CHUNK)
         quantise_w2(1)
         quantise_z(1, 0, CHUNK)
-        last_slope(1, "w2_bf1")
+        last_slope(1, "slot_s")
         second_product(1, 0, CHUNK)
         quantise_z(0, CHUNK, CHUNK)
         quantise_z(1, CHUNK, CHUNK)

@@ -26,6 +26,7 @@ SLICES = S // BANK
 N_TILES = N // P
 CHUNK = 256
 CHUNKS = M // CHUNK
+SPARE = P - 16
 ACC_BANKS = 6
 
 
@@ -41,8 +42,8 @@ def tile_list_soft_datalog_firing_kernel(
 
         facts = lists.tile([P, S // 16], U16, name="facts")
         atoms = lists.tile([P, M // 16], U16, name="atoms")
-        w1_w = ring.tile([P, H], U16, name="w1_w", tag="slot_b", align_bytes=64)
-        w1_s = ring.tile([P, H], U8, name="w1_s", tag="slot_d", align_bytes=64)
+        w1_w = ring.tile([P, H], U16, name="w1_w", tag="z_b", align_bytes=64)
+        w1_s = ring.tile([P, H], U8, name="w1_s", tag="z_a", align_bytes=64)
         tab_s = ring.tile([P, T], U8, name="tab_s", tag="slot_c", align_bytes=64)
         w1p_w = keep.tile([P, 2 * H], U8, name="w1p_w", align_bytes=64)
         w1p_s = keep.tile([P, H], U8, name="w1p_s", align_bytes=64)
@@ -53,23 +54,24 @@ def tile_list_soft_datalog_firing_kernel(
         w2_s = keep.tile([P, PASSES, N], U8, name="w2_s", align_bytes=64)
         z_w = keep.tile([P, PASSES, M], U32, name="z_w", align_bytes=64)
         z_s = keep.tile([P, PASSES, M], U8, name="z_s", align_bytes=64)
+        gain_sb = keep.tile([P, PLANES], F32, name="gain_sb")
         warm = keep.tile([P, 1], F32, name="warm")
-        zeros = [ring.tile([P, H // 8], I32, name="zeros", tag=tag, align_bytes=64) for tag in ("slot_a", "slot_w")]
+        zeros = ring.tile([P, H // 4], I32, name="zeros", tag="slot_w", align_bytes=64)
 
-        nc.gpsimd.memset(tab_s[:, : T // 2].bitcast(I32), 0)
-        for u in range(2):
-            nc.gpsimd.memset(zeros[u][:], 0)
-        nc.vector.memset(tab_s[:, T // 2 :].bitcast(I32), 0)
-        for u in range(2):
-            nc.vector.tensor_copy(w1_s[:, u * H // 2 : (u + 1) * H // 2].bitcast(I32), zeros[u][:])
+        nc.gpsimd.memset(zeros[:], 0)
+        nc.vector.memset(tab_s[:SPARE, :].bitcast(I32), 0)
+        nc.vector.tensor_copy(w1_s[:].bitcast(I32), zeros[:])
         make_identity(nc, ident[:])
         nc.gpsimd.memset(v_s[:].bitcast(I32), 0)
         nc.scalar.activation(warm[:], ident[:, 0:1], ACT.Sigmoid)
 
-        nc.sync.dma_start(w1_w[:].bitcast(I32), w1_words[0].bitcast(I32))
+        nc.sync.dma_start(tab_s[SPARE:, :].bitcast(I32), tab_scales[0].bitcast(I32))
         nc.sync.dma_start(facts[:], offs)
+        nc.sync.dma_start(w1_w[:].bitcast(I32), w1_words[0].bitcast(I32))
+        nc.sync.dma_start(
+            gain_sb[:].rearrange("p (b i) -> p b i", i=PACK), gain.rearrange("(b p i) -> p b i", p=P, i=PACK)
+        )
         nc.sync.dma_start(atoms[:], offs2)
-        nc.sync.dma_start(tab_s[0:P:8, :].bitcast(I32), tab_scales[0].bitcast(I32))
 
         tab_w = ring.tile([P, T], U32, name="tab_w", tag="slot_a", align_bytes=64)
         nc.sync.dma_start(tab_w[:].bitcast(I32), tab_words[0].rearrange("p t i -> p (t i)").bitcast(I32))
@@ -79,36 +81,34 @@ def tile_list_soft_datalog_firing_kernel(
                 w1_scales[0, 4 * quad : 4 * quad + 4, :].bitcast(I32),
             )
 
-        nc.vector.tensor_copy(
+        nc.scalar.copy(
             w1p_w[:].bitcast(U16).rearrange("p (b i m) -> p b i m", b=PASSES, i=PACK),
             w1_w[:].rearrange("p (b m i) -> p b i m", b=PASSES, i=PACK),
         )
         nc.vector.tensor_copy(spread_s[:], tab_s[:].indirect(facts[:]))
-        nc.vector.tensor_copy(
+        nc.gpsimd.tensor_copy(
             w1p_s[:].rearrange("p (b i m) -> p b i m", b=PASSES, i=PACK),
             w1_s[:].rearrange("p (b m i) -> p b i m", b=PASSES, i=PACK),
         )
 
-        early = ring.tile([P, PLANES + M], F32, name="early", tag="slot_w", align_bytes=64)
-        gain_sb = early[:, 0:PLANES]
+        early = ring.tile([P, 2 * M], F32, name="early", tag="slot_w", align_bytes=64)
+        wgt_sb = early[:, :M]
         c_view = c.rearrange("(b p i) m -> b p i m", p=P, i=PACK)
         w2_view = w2.rearrange("(b p i) n -> b p i n", p=P, i=PACK)
 
-        wgt_sb = early[:, PLANES:]
         nc.sync.dma_start(wgt_sb, wgt)
-        nc.sync.dma_start(
-            gain_sb.rearrange("p (b i) -> p b i", i=PACK), gain.rearrange("(b p i) -> p b i", p=P, i=PACK)
-        )
-        for row in range(4):
-            nc.sync.dma_start(v_s[row:P:32, :].bitcast(I32), spread_s[8 * row : P : 32, :].bitcast(I32))
+        nc.sync.dma_start(early[:, M:], c_view[0, :, 0, :])
 
-        late = ring.tile([P, PLANES * M + PACK * N + N_TILES], F32, name="late", tag="slot_c", align_bytes=64)
-        prior = [late[:, q * M : (q + 1) * M] for q in range(PLANES)]
-        prior1 = late[:, PACK * M : PLANES * M].rearrange("p (i m) -> p i m", i=PACK)
+        held = PLANES - 1
+        late = ring.tile([P, held * M + PACK * N + N_TILES], F32, name="late", tag="slot_c", align_bytes=64)
+        prior = [early[:, M:]] + [late[:, q * M : (q + 1) * M] for q in range(held)]
+        prior1 = late[:, (held - PACK) * M : held * M].rearrange("p (i m) -> p i m", i=PACK)
         w2_last = ring.tile([P, PACK, N], F32, name="w2_last", tag="slot_s", align_bytes=64)
-        w2_raw = [late[:, PLANES * M : PLANES * M + PACK * N].rearrange("p (i n) -> p i n", i=PACK), w2_last[:]]
-        bias_sb = late[:, PLANES * M + PACK * N :]
-        for q in range(PLANES):
+        w2_raw = [late[:, held * M : held * M + PACK * N].rearrange("p (i n) -> p i n", i=PACK), w2_last[:]]
+        bias_sb = late[:, held * M + PACK * N :]
+        for row in range(4):
+            nc.sync.dma_start(v_s[row:P:32, :].bitcast(I32), spread_s[SPARE + row : P : 4, :].bitcast(I32))
+        for q in range(1, PLANES):
             nc.sync.dma_start(prior[q], c_view[q // PACK, :, q % PACK, :])
         with nc.allow_non_contiguous_dma(reason="one bias value a partition"):
             nc.sync.dma_start(bias_sb, bias.rearrange("(t p) -> p t", p=P))

@@ -27,6 +27,7 @@ N_TILES = N // P
 CHUNK = 256
 CHUNKS = M // CHUNK
 SPARE = P - 16
+WINDOWS = 6
 ACC_BANKS = 6
 
 
@@ -137,14 +138,13 @@ def tile_list_soft_datalog_firing_kernel(
             for k in range(PACK):
                 nc.tensor.transpose(wgt_ps[h][:, k * P : (k + 1) * P], across[h][:, k * P : (k + 1) * P], ident[:])
 
-        for q in range(PACK):
-            nc.gpsimd.tensor_scalar(prior[q], prior[q], gain_sb[:, q : q + 1], 0.0, ALU.mult, ALU.add)
-
-        def priors_of_pass_1():
-            zero = ring.tile([P, 1], F32, name="zero", tag="slope0", align_bytes=64)
-            nc.gpsimd.memset(zero[:], 0.0)
-            for q in range(PACK, PLANES):
-                nc.gpsimd.tensor_scalar(prior[q], prior[q], gain_sb[:, q : q + 1], zero[:], ALU.mult, ALU.add)
+        zero = ring.tile([P, 1], F32, name="zero", tag="picked0", align_bytes=64)
+        nc.gpsimd.memset(zero[:], 0.0)
+        for q in range(PLANES - 1):
+            nc.gpsimd.tensor_scalar(prior[q], prior[q], gain_sb[:, q : q + 1], zero[:], ALU.mult, ALU.add)
+        for h, nothing in enumerate((zero[:], 0.0)):
+            half = prior[PLANES - 1][:, h * BANK : (h + 1) * BANK]
+            nc.gpsimd.tensor_scalar(half, half, gain_sb[:, PLANES - 1 :], nothing, ALU.mult, ALU.add)
 
         v_first = keep.tile([P, BANK], U32, name="v_first", align_bytes=64)
         v_rest = ring.tile([P, (SLICES - 1) * BANK], U32, name="v_rest", tag="slot_d", align_bytes=64)
@@ -158,7 +158,7 @@ def tile_list_soft_datalog_firing_kernel(
 
         def first_product(q, s):
             if s == 0:
-                truth[q] = ring.tile([P, S], F32, name="truth", tag="window%d" % q, align_bytes=64)
+                truth[q] = ring.tile([P, S], F32, name="truth", tag="window%d" % (q % WINDOWS), align_bytes=64)
             acc = bank("acc")
             nc.tensor.matmul_mx(
                 out=acc[:],
@@ -177,10 +177,9 @@ def tile_list_soft_datalog_firing_kernel(
 
         slopes = {}
 
-        reused = {2: "window0", 3: "window1", 4: "slope1"}
 
         def slope(q):
-            slopes[q] = ring.tile([P, M], F32, name="slope", tag=reused.get(q, "slope%d" % q), align_bytes=64)
+            slopes[q] = ring.tile([P, M], F32, name="slope", tag="slope%d" % q, align_bytes=64)
             for h in range(M // BANK):
                 half = slice(h * BANK, (h + 1) * BANK)
                 nc.vector.scalar_tensor_tensor(
@@ -200,9 +199,9 @@ def tile_list_soft_datalog_firing_kernel(
                 ALU.mult,
             )
 
-        pairs0 = [ring.tile([P, 2, M], F32, name="picked0", tag="pair%d" % u, align_bytes=64) for u in range(2)]
         picked1 = keep.tile([P, PACK, M], F32, name="picked1")
-        picked = [pairs0[q // 2][:, q % 2, :] for q in range(PACK)] + [picked1[:, i, :] for i in range(PACK)]
+        picked0 = ring.tile([P, PACK, M], F32, name="picked0", tag="picked0", align_bytes=64)
+        picked = [picked0[:, i, :] for i in range(PACK)] + [picked1[:, i, :] for i in range(PACK)]
 
         def pick(q):
             nc.vector.tensor_tensor(picked[q], truth[q][:].indirect(atoms[:]), slopes[q][:], ALU.mult)
@@ -343,46 +342,52 @@ def tile_list_soft_datalog_firing_kernel(
         wgt_forward(0)
         wgt_forward(1)
         first_product(0, 0)
-        wgt_backward(0)
-        wgt_backward(1)
-        for s in range(1, SLICES):
-            first_product(0, s)
-        slope(0)
-        slope(1)
-        truth_plane(1)
-        pick(0)
-        priors_of_pass_1()
-        truth_plane(2)
-        pick(1)
-        for q in range(2, PLANES - 1):
+        first_product(0, 1)
+        for h in range(2):
+            wgt_backward(h)
+            first_product(1, h)
+            first_product(0, 2 + h)
+        for q in range(PLANES - 1):
             slope(q)
         last_slope(0, "slope_a")
+        for s in range(2, SLICES):
+            first_product(1, s)
+        pick(0)
+        truth_plane(2)
+        pick(1)
         truth_plane(3)
         pick(2)
+        round_w2(0)
 
-        def plane_with_forward(q, j):
-            first_product(q, 0)
-            first_product(q, 1)
-            forward(0, j)
-            first_product(q, 2)
-            first_product(q, 3)
+        def plane_with_forward(q, g, chunks):
+            for half in range(2):
+                first_product(q, 2 * half)
+                first_product(q, 2 * half + 1)
+                for j in chunks[half : half + 1]:
+                    forward(g, j)
 
         new_rounded(0)
-        for j in range(CHUNKS):
-            plane_with_forward(PACK + j, j)
-            pick(PACK - 1 + j)
+        truth_plane(4)
+        pick(3)
+        plane_with_forward(5, 0, [0, 1])
+        pick(4)
+        plane_with_forward(6, 0, [2, 3])
+        pick(5)
         new_rounded(1)
-        for j in range(CHUNKS):
-            forward(1, j)
+        plane_with_forward(7, 1, [0, 1])
+        pick(6)
 
-        new_z(0, 0, CHUNKS, "pair0")
+        new_z(0, 0, 2, "z_0")
+        new_z(0, 2, 2, "z_1")
         new_z(1, 0, 1, "z_a")
         new_z(1, 1, 1, "z_b")
-        round_w2(0)
         backward(0)
+        backward(1)
         round_w2(1)
-        for j in range(1, CHUNKS):
-            backward(j)
+        forward(1, 2)
+        forward(1, 3)
+        backward(2)
+        backward(3)
         pick_last(0)
         pick_last(1)
         join_on_vector(0, CHUNK)
@@ -408,7 +413,7 @@ def tile_list_soft_datalog_firing_kernel(
         for h in range(2):
             open_piece(3 * CHUNK + h * P, h)
             second_product(0, 3 * CHUNK + h * P, P)
-        new_z(1, 2, 1, "pair0")
+        new_z(1, 2, 1, "z_1")
         join_on_vector(2 * CHUNK, CHUNK)
         pick_last(3)
         quantise_z(1, 2 * CHUNK, CHUNK)

@@ -120,9 +120,15 @@ def tile_list_soft_datalog_firing_kernel(
 
         turns = []
 
-        def bank(name):
-            turns.append(name)
-            return psum.tile([P, BANK], F32, name=name, tag="acc%d" % (len(turns) % ACC_BANKS))
+        tag_of = {"wgt0": "wgt_ps0", "wgt1": "wgt_ps1"}
+
+        def bank(name, after=None):
+            if after is None:
+                turns.append(name)
+                tag_of[name] = "acc%d" % (len(turns) % ACC_BANKS)
+            else:
+                tag_of[name] = tag_of[after]
+            return psum.tile([P, BANK], F32, name="bank", tag=tag_of[name])
 
         across = {}
 
@@ -131,7 +137,7 @@ def tile_list_soft_datalog_firing_kernel(
             for k in range(PACK):
                 m0 = h * BANK + k * P
                 nc.tensor.transpose(turned[:, k * P : (k + 1) * P], wgt_sb[:, m0 : m0 + P], ident[:])
-            across[h] = ring.tile([P, BANK], F32, name="across", tag="rounded%d" % h)
+            across[h] = ring.tile([P, BANK], F32, name="across", tag="rounded%d0" % h, align_bytes=64)
             nc.scalar.activation(across[h][:], turned[:], ACT.Copy, scale=-1.0)
 
         def wgt_backward(h):
@@ -159,7 +165,7 @@ def tile_list_soft_datalog_firing_kernel(
         def first_product(q, s):
             if s == 0:
                 truth[q] = ring.tile([P, S], F32, name="truth", tag="window%d" % (q % WINDOWS), align_bytes=64)
-            acc = bank("acc")
+            acc = bank("acc%d%d" % (q, s))
             nc.tensor.matmul_mx(
                 out=acc[:],
                 lhsT=w1p_w[:, 2 * P * q : 2 * P * (q + 1)].bitcast(FP4X4),
@@ -186,56 +192,66 @@ def tile_list_soft_datalog_firing_kernel(
                     slopes[q][:, half], prior[q][:, half], gain_sb[:, q : q + 1], wgt_ps[h][:], ALU.subtract, ALU.mult
                 )
 
-        last_slopes = {}
-
-        def last_slope(h, tag):
-            last_slopes[h] = ring.tile([P, BANK], F32, name="last_slope", tag=tag, align_bytes=64)
-            nc.vector.scalar_tensor_tensor(
-                last_slopes[h][:],
-                prior[PLANES - 1][:, h * BANK : (h + 1) * BANK],
-                gain_sb[:, PLANES - 1 : PLANES],
-                wgt_ps[h][:],
-                ALU.subtract,
-                ALU.mult,
-            )
-
-        picked1 = keep.tile([P, PACK, M], F32, name="picked1")
         picked0 = ring.tile([P, PACK, M], F32, name="picked0", tag="picked0", align_bytes=64)
-        picked = [picked0[:, i, :] for i in range(PACK)] + [picked1[:, i, :] for i in range(PACK)]
+        picked1 = {}
 
-        def pick(q):
-            nc.vector.tensor_tensor(picked[q], truth[q][:].indirect(atoms[:]), slopes[q][:], ALU.mult)
+        def picked(q, m0, width):
+            if q < PACK:
+                return picked0[:, q, m0 : m0 + width]
+            tile, first = picked1[m0 // CHUNK]
+            return tile[:, q - PACK, m0 - first : m0 - first + width]
 
-        def pick_last(j):
-            h, part = divmod(j, BANK // CHUNK)
+        def pick(q, m0=0, width=M):
             nc.vector.tensor_tensor(
-                picked[PLANES - 1][:, j * CHUNK : (j + 1) * CHUNK],
-                truth[PLANES - 1][:].indirect(atoms[:, j * CHUNK // 16 : (j + 1) * CHUNK // 16]),
-                last_slopes[h][:, part * CHUNK : (part + 1) * CHUNK],
+                picked(q, m0, width),
+                truth[q][:].indirect(atoms[:, m0 // 16 : (m0 + width) // 16]),
+                slopes[q][:, m0 : m0 + width],
                 ALU.mult,
             )
+
+        def new_picked(j, chunks, tag):
+            tile = ring.tile([P, PACK, CHUNK * chunks], F32, name="picked1", tag=tag, align_bytes=64)
+            for k in range(chunks):
+                picked1[j + k] = (tile, j * CHUNK)
+
+        def pick_run(j, chunks, tag):
+            new_picked(j, chunks, tag)
+            for q in range(PACK, PLANES):
+                pick(q, j * CHUNK, chunks * CHUNK)
 
         rounded = {}
 
-        def new_rounded(g):
-            rounded[g] = ring.tile([P, 2 * M], BF16, name="rounded", tag="rounded%d" % g)
+        def new_rounded(g, j, chunks, tag):
+            tile = ring.tile([P, 2 * CHUNK * chunks], BF16, name="rounded", tag=tag, align_bytes=64)
+            for k in range(chunks):
+                rounded[g, j + k] = (tile, j * CHUNK)
 
-        def forward(g, j):
-            turned = bank("turned")
+        turned = {}
+
+        def turn(g, j, after=None):
+            turned[g, j] = bank("turned%d%d" % (g, j), after)
             for k in range(CHUNK // P):
                 m0 = j * CHUNK + k * P
                 for e in range(2):
-                    dst = turned[:, (2 * k + e) * P : (2 * k + e + 1) * P]
+                    dst = turned[g, j][:, (2 * k + e) * P : (2 * k + e + 1) * P]
                     nc.tensor.matmul(
                         dst, prior[2 * g + e][:, m0 : m0 + P], ident[:], start=True, stop=False, is_transpose=True
                     )
                     nc.tensor.matmul(
-                        dst, picked[2 * g + e][:, m0 : m0 + P], ident[:], start=False, stop=True, is_transpose=True
+                        dst, picked(2 * g + e, m0, P), ident[:], start=False, stop=True, is_transpose=True
                     )
+
+        def round_pair(g, j):
+            tile, first = rounded[g, j]
+            m0 = j * CHUNK - first
             nc.scalar.copy(
-                rounded[g][:, 2 * j * CHUNK : 2 * (j + 1) * CHUNK].rearrange("m (k p e) -> m k p e", k=2, e=2),
-                turned[:].rearrange("m (k e p) -> m k p e", k=2, e=2),
+                tile[:, 2 * m0 : 2 * (m0 + CHUNK)].rearrange("m (k p e) -> m k p e", k=2, e=2),
+                turned[g, j][:].rearrange("m (k e p) -> m k p e", k=2, e=2),
             )
+
+        def forward(g, j, after=None):
+            turn(g, j, after)
+            round_pair(g, j)
 
         zs = {}
 
@@ -248,23 +264,24 @@ def tile_list_soft_datalog_firing_kernel(
             tile, first = zs[b, m0 // CHUNK]
             return tile[:, PACK * (m0 - first) : PACK * (m0 - first + width)]
 
-        def backward(j):
-            back = bank("back")[:].rearrange("p (k u m) -> p k u m", u=2, m=P)
+        def backward(b, j, after):
+            back = bank("back%d%d" % (b, j), after)[:].rearrange("p (k u m) -> p k u m", u=2, m=P)
             for k in range(CHUNK // P):
-                m0 = j * CHUNK + k * P
                 for u in range(2):
-                    words = rounded[u][:].bitcast(F32)
-                    nc.tensor.transpose(back[:, k, u, :], words[:, m0 : m0 + P], ident[:])
+                    tile, first = rounded[2 * b + u, j]
+                    m0 = j * CHUNK + k * P - first
+                    nc.tensor.transpose(back[:, k, u, :], tile[:].bitcast(F32)[:, m0 : m0 + P], ident[:])
             nc.scalar.copy(
-                z_cols(0, j * CHUNK, CHUNK).bitcast(F32).rearrange("p (k m u) -> p k m u", u=2, m=P),
+                z_cols(b, j * CHUNK, CHUNK).bitcast(F32).rearrange("p (k m u) -> p k m u", u=2, m=P),
                 back.rearrange("p k u m -> p k m u"),
             )
 
         def join_on_vector(m0, width):
+            tile, first = picked1[m0 // CHUNK]
             nc.vector.tensor_tensor(
                 z_cols(1, m0, width).rearrange("p (c e i) -> p c i e", e=2, i=PACK),
                 prior1[:, :, m0 : m0 + width].rearrange("p i (c e) -> p c i e", e=2),
-                picked1[:, :, m0 : m0 + width].rearrange("p i (c e) -> p c i e", e=2),
+                tile[:, :, m0 - first : m0 - first + width].rearrange("p i (c e) -> p c i e", e=2),
                 ALU.add,
             )
 
@@ -278,8 +295,8 @@ def tile_list_soft_datalog_firing_kernel(
 
         w2_bf = {}
 
-        def round_w2(b):
-            w2_bf[b] = ring.tile([P, N * PACK], BF16, name="w2_bf", tag="w2_bf%d" % b, align_bytes=64)
+        def round_w2(b, tag):
+            w2_bf[b] = ring.tile([P, N * PACK], BF16, name="w2_bf", tag=tag, align_bytes=64)
             nc.scalar.copy(
                 w2_bf[b][:].rearrange("p (c e i) -> p c i e", e=2, i=PACK),
                 w2_raw[b].rearrange("p i (c e) -> p c i e", e=2),
@@ -292,14 +309,14 @@ def tile_list_soft_datalog_firing_kernel(
 
         evidence = {}
 
-        def open_chunk(m0):
+        def open_chunk(m0, after):
             for u in range(2):
-                tile = bank("evidence")
+                tile = bank("evidence%d_%d" % (m0, u), after[u])
                 for half in range(2):
                     evidence[m0, 2 * u + half] = (tile[:, half * CHUNK : (half + 1) * CHUNK], half == 0, half == 1)
 
-        def open_piece(m0, h):
-            tiles = [psum.tile([P, BANK], F32, name="evidence", tag="wgt_ps%d" % h), bank("evidence")]
+        def open_piece(m0, after):
+            tiles = [bank("evidence%d_%d" % (m0, u), after[u]) for u in range(2)]
             for t in range(N_TILES):
                 u, half = divmod(t, 2)
                 evidence[m0, t] = (tiles[u][:, half * P : (half + 1) * P], half == 0, half == 1)
@@ -318,17 +335,10 @@ def tile_list_soft_datalog_firing_kernel(
                     stop=(b == PASSES - 1 and closes),
                 )
 
-        def store_chunk(m0):
-            cols = slice(m0, m0 + CHUNK)
+        def store(m0, width, on_scalar):
+            cols = slice(m0, m0 + width)
             for t in range(N_TILES):
-                nc.scalar.activation(res[:, t, cols], evidence[m0, t][0], ACT.Identity, bias=bias_sb[:, t : t + 1])
-                if t % 2 == 1:
-                    nc.sync.dma_start(out_view[:, t - 1 : t + 1, cols], res[:, t - 1 : t + 1, cols])
-
-        def store_piece(m0):
-            cols = slice(m0, m0 + P)
-            for t in range(N_TILES):
-                if t < N_TILES // 2:
+                if t < on_scalar:
                     nc.scalar.activation(
                         res[:, t, cols], evidence[m0, t][0], ACT.Identity, bias=bias_sb[:, t : t + 1]
                     )
@@ -347,9 +357,8 @@ def tile_list_soft_datalog_firing_kernel(
             wgt_backward(h)
             first_product(1, h)
             first_product(0, 2 + h)
-        for q in range(PLANES - 1):
+        for q in range(PLANES):
             slope(q)
-        last_slope(0, "slope_a")
         for s in range(2, SLICES):
             first_product(1, s)
         pick(0)
@@ -357,74 +366,76 @@ def tile_list_soft_datalog_firing_kernel(
         pick(1)
         truth_plane(3)
         pick(2)
-        round_w2(0)
-
-        def plane_with_forward(q, g, chunks):
-            for half in range(2):
-                first_product(q, 2 * half)
-                first_product(q, 2 * half + 1)
-                for j in chunks[half : half + 1]:
-                    forward(g, j)
-
-        new_rounded(0)
+        round_w2(0, "w2_bf0")
         truth_plane(4)
         pick(3)
-        plane_with_forward(5, 0, [0, 1])
-        pick(4)
-        plane_with_forward(6, 0, [2, 3])
-        pick(5)
-        new_rounded(1)
-        plane_with_forward(7, 1, [0, 1])
-        pick(6)
+        truth_plane(5)
+        for g in range(2):
+            new_rounded(g, 0, 2, "rounded%d0" % g)
+        turn(0, 2, "wgt0")
+        turn(0, 3, "wgt1")
+        for q in (6, 7):
+            first_product(q, 0)
+            first_product(q, 1)
+            forward(0, q - 6)
+            first_product(q, 2)
+            first_product(q, 3)
+        pick_run(0, 2, "picked1a")
+        quantise_w2(0)
 
         new_z(0, 0, 2, "z_0")
         new_z(0, 2, 2, "z_1")
         new_z(1, 0, 1, "z_a")
         new_z(1, 1, 1, "z_b")
-        backward(0)
-        backward(1)
-        round_w2(1)
-        forward(1, 2)
-        forward(1, 3)
-        backward(2)
-        backward(3)
-        pick_last(0)
-        pick_last(1)
-        join_on_vector(0, CHUNK)
+        forward(1, 0)
+        forward(1, 1)
+        for g in range(2):
+            new_rounded(g, 2, 2, "rounded%d1" % g)
+            new_rounded(2 + g, 0, 1, "slope%d" % g)
+        round_pair(0, 2)
+        round_pair(0, 3)
+        backward(0, 0, "acc72")
+        backward(0, 1, "acc73")
+        round_w2(1, "rounded00")
         join_on_vector(CHUNK, CHUNK)
-        quantise_w2(0)
-        quantise_z(0, 0, CHUNK)
-        open_chunk(0)
-        second_product(0, 0, CHUNK)
+        pick_run(2, 1, "picked1b")
+        new_z(1, 2, 1, "slope2")
+        join_on_vector(2 * CHUNK, CHUNK)
+        forward(1, 2, "turned10")
+        forward(1, 3, "turned11")
+        forward(2, 0, "turned02")
+        forward(3, 0, "turned03")
+        backward(0, 2, "acc71")
+        backward(0, 3, "turned01")
+        backward(1, 0, "back00")
+        quantise_z(0, 0, 2 * CHUNK)
         quantise_w2(1)
-        quantise_z(1, 0, CHUNK)
-        last_slope(1, "slot_s")
-        second_product(1, 0, CHUNK)
-        quantise_z(0, CHUNK, CHUNK)
         quantise_z(1, CHUNK, CHUNK)
-        open_chunk(CHUNK)
+        open_chunk(CHUNK, ("back01", "turned12"))
         second_product(0, CHUNK, CHUNK)
         second_product(1, CHUNK, CHUNK)
-        store_chunk(0)
-        pick_last(2)
-        quantise_z(0, 2 * CHUNK, 2 * CHUNK)
-        open_chunk(2 * CHUNK)
-        second_product(0, 2 * CHUNK, CHUNK)
-        for h in range(2):
-            open_piece(3 * CHUNK + h * P, h)
-            second_product(0, 3 * CHUNK + h * P, P)
-        new_z(1, 2, 1, "z_1")
-        join_on_vector(2 * CHUNK, CHUNK)
-        pick_last(3)
         quantise_z(1, 2 * CHUNK, CHUNK)
-        store_chunk(CHUNK)
+        quantise_z(0, 2 * CHUNK, 2 * CHUNK)
+        open_chunk(2 * CHUNK, ("turned13", "turned20"))
+        second_product(0, 2 * CHUNK, CHUNK)
         second_product(1, 2 * CHUNK, CHUNK)
+        store(CHUNK, CHUNK, N_TILES)
+        open_chunk(0, ("turned30", "back02"))
+        second_product(0, 0, CHUNK)
+        open_piece(3 * CHUNK, ("back03", "back10"))
+        second_product(0, 3 * CHUNK, P)
+        open_piece(3 * CHUNK + P, ("evidence%d_0" % CHUNK, "evidence%d_1" % CHUNK))
+        second_product(0, 3 * CHUNK + P, P)
+        quantise_z(1, 0, CHUNK)
+        second_product(1, 0, CHUNK)
+        store(2 * CHUNK, CHUNK, N_TILES)
+        pick_run(3, 1, "slope0")
         new_z(1, 3, 1, "z_b")
         for h in range(2):
             join_on_vector(3 * CHUNK + h * P, P)
-        store_chunk(2 * CHUNK)
+        store(0, CHUNK, N_TILES)
         for h in range(2):
             quantise_z(1, 3 * CHUNK + h * P, P)
             second_product(1, 3 * CHUNK + h * P, P)
         for h in range(2):
-            store_piece(3 * CHUNK + h * P)
+            store(3 * CHUNK + h * P, P, N_TILES // 2)

@@ -45,11 +45,11 @@ def tile_list_soft_datalog_firing_kernel(
         atoms = lists.tile([P, M // 16], U16, name="atoms")
         w1_w = ring.tile([P, H], U16, name="w1_w", tag="z_b", align_bytes=64)
         w1_s = ring.tile([P, H], U8, name="w1_s", tag="z_a", align_bytes=64)
-        tab_s = ring.tile([P, T], U8, name="tab_s", tag="slot_c", align_bytes=64)
+        tab_s = ring.tile([P, T], U8, name="tab_s", tag="slot_c", align_bytes=256)
         w1p_w = keep.tile([P, 2 * H], U8, name="w1p_w", align_bytes=64)
         w1p_s = keep.tile([P, H], U8, name="w1p_s", align_bytes=64)
         v_s = keep.tile([P, S], U8, name="v_s", align_bytes=64)
-        spread_s = ring.tile([P, S], U8, name="spread_s", tag="slot_s", align_bytes=64)
+        spread_s = ring.tile([P, S], U8, name="spread_s", tag="slot_s", align_bytes=256)
         ident = keep.tile([P, P], F32, name="ident")
         w2_w = keep.tile([P, PASSES, N], U32, name="w2_w", align_bytes=64)
         w2_s = keep.tile([P, PASSES, N], U8, name="w2_s", align_bytes=64)
@@ -57,7 +57,7 @@ def tile_list_soft_datalog_firing_kernel(
         z_s = keep.tile([P, PASSES, M], U8, name="z_s", align_bytes=64)
         gain_sb = keep.tile([P, PLANES], F32, name="gain_sb")
         warm = keep.tile([P, 1], F32, name="warm")
-        zeros = ring.tile([P, H // 4], I32, name="zeros", tag="slot_w", align_bytes=64)
+        zeros = ring.tile([P, H // 4], I32, name="zeros", tag="slot_w", align_bytes=256)
 
         nc.gpsimd.memset(zeros[:], 0)
         nc.vector.memset(tab_s[:SPARE, :].bitcast(I32), 0)
@@ -74,7 +74,7 @@ def tile_list_soft_datalog_firing_kernel(
         )
         nc.sync.dma_start(atoms[:], offs2)
 
-        tab_w = ring.tile([P, T], U32, name="tab_w", tag="slot_a", align_bytes=64)
+        tab_w = ring.tile([P, T], U32, name="tab_w", tag="slot_a", align_bytes=256)
         nc.sync.dma_start(tab_w[:].bitcast(I32), tab_words[0].rearrange("p t i -> p (t i)").bitcast(I32))
         for quad in range(4):
             nc.sync.dma_start(
@@ -92,7 +92,7 @@ def tile_list_soft_datalog_firing_kernel(
             w1_s[:].rearrange("p (b m i) -> p b i m", b=PASSES, i=PACK),
         )
 
-        early = ring.tile([P, 2 * M], F32, name="early", tag="slot_w", align_bytes=64)
+        early = ring.tile([P, 2 * M], F32, name="early", tag="slot_w", align_bytes=256)
         wgt_sb = early[:, :M]
         c_view = c.rearrange("(b p i) m -> b p i m", p=P, i=PACK)
         w2_view = w2.rearrange("(b p i) n -> b p i n", p=P, i=PACK)
@@ -101,10 +101,10 @@ def tile_list_soft_datalog_firing_kernel(
         nc.sync.dma_start(early[:, M:], c_view[0, :, 0, :])
 
         held = PLANES - 1
-        late = ring.tile([P, held * M + PACK * N + N_TILES], F32, name="late", tag="slot_c", align_bytes=64)
+        late = ring.tile([P, held * M + PACK * N + N_TILES], F32, name="late", tag="slot_c", align_bytes=256)
         prior = [early[:, M:]] + [late[:, q * M : (q + 1) * M] for q in range(held)]
         prior1 = late[:, (held - PACK) * M : held * M].rearrange("p (i m) -> p i m", i=PACK)
-        w2_last = ring.tile([P, PACK, N], F32, name="w2_last", tag="slot_s", align_bytes=64)
+        w2_last = ring.tile([P, PACK, N], F32, name="w2_last", tag="slot_s", align_bytes=256)
         w2_raw = [late[:, held * M : held * M + PACK * N].rearrange("p (i n) -> p i n", i=PACK), w2_last[:]]
         bias_sb = late[:, held * M + PACK * N :]
         for row in range(4):
@@ -158,7 +158,7 @@ def tile_list_soft_datalog_firing_kernel(
         for s in range(SLICES):
             nc.vector.tensor_copy(v_w[s], tab_w[:].indirect(facts[:, s * BANK // 16 : (s + 1) * BANK // 16]))
 
-        res = ring.tile([P, N_TILES, M], F32, name="res", tag="slot_a", align_bytes=64)
+        res = ring.tile([P, N_TILES, M], F32, name="res", tag="slot_a", align_bytes=256)
 
         truth = {}
 

from contextlib import ExitStack

import concourse.mybir as mybir
from concourse.masks import make_identity

K, T, S, M, H, N = 512, 4096, 2048, 1024, 1024, 512
FLOPS = 2 * K * H * S + 2 * H * N * M

F32 = mybir.dt.float32
BF16 = mybir.dt.bfloat16
I32 = mybir.dt.int32
U32 = mybir.dt.uint32
U16 = mybir.dt.uint16
U8 = mybir.dt.uint8
FP8X4 = mybir.dt.float8_e4m3fn_x4
FP4X4 = mybir.dt.float4_e2m1fn_x4
ALU = mybir.AluOpType
ACT = mybir.ActivationFunctionType

P = 128
PACK = 4
BANK = 512
PASSES = H // (P * PACK)
PLANES = PASSES * PACK
SLICES = S // BANK
N_TILES = N // P
CHUNK = 256
CHUNKS = M // CHUNK
SPARE = P - 16
WINDOWS = 6
ACC_BANKS = 6


def tile_list_soft_datalog_firing_kernel(
    tc, tab_words, tab_scales, offs, w1_words, w1_scales, offs2, wgt, c, gain, w2, bias, out
):
    nc = tc.nc
    with ExitStack() as ctx:
        lists = ctx.enter_context(tc.tile_pool(name="lists", bufs=1))
        keep = ctx.enter_context(tc.tile_pool(name="keep", bufs=1))
        ring = ctx.enter_context(tc.tile_pool(name="ring", bufs=1))
        psum = ctx.enter_context(tc.psum_pool(name="psum", bufs=1))

        facts = lists.tile([P, S // 16], U16, name="facts")
        atoms = lists.tile([P, M // 16], U16, name="atoms")
        w1_w = ring.tile([P, H], U16, name="w1_w", tag="z_b", align_bytes=64)
        w1_s = ring.tile([P, H], U8, name="w1_s", tag="z_a", align_bytes=64)
        tab_s = ring.tile([P, T], U8, name="tab_s", tag="slot_c", align_bytes=256)
        w1p_w = keep.tile([P, 2 * H], U8, name="w1p_w", align_bytes=64)
        w1p_s = keep.tile([P, H], U8, name="w1p_s", align_bytes=64)
        v_s = keep.tile([P, S], U8, name="v_s", align_bytes=64)
        spread_s = ring.tile([P, S], U8, name="spread_s", tag="slot_s", align_bytes=256)
        ident = keep.tile([P, P], F32, name="ident")
        w2_w = keep.tile([P, PASSES, N], U32, name="w2_w", align_bytes=64)
        w2_s = keep.tile([P, PASSES, N], U8, name="w2_s", align_bytes=64)
        z_w = keep.tile([P, PASSES, M], U32, name="z_w", align_bytes=64)
        z_s = keep.tile([P, PASSES, M], U8, name="z_s", align_bytes=64)
        gain_sb = keep.tile([P, PLANES], F32, name="gain_sb")
        warm = keep.tile([P, 1], F32, name="warm")
        zeros = ring.tile([P, H // 4], I32, name="zeros", tag="slot_w", align_bytes=256)

        nc.gpsimd.memset(zeros[:], 0)
        nc.vector.memset(tab_s[:SPARE, :].bitcast(I32), 0)
        nc.vector.tensor_copy(w1_s[:].bitcast(I32), zeros[:])
        make_identity(nc, ident[:])
        nc.gpsimd.memset(v_s[:].bitcast(I32), 0)
        nc.scalar.activation(warm[:], ident[:, 0:1], ACT.Sigmoid)

        nc.sync.dma_start(tab_s[SPARE:, :].bitcast(I32), tab_scales[0].bitcast(I32))
        nc.sync.dma_start(facts[:], offs)
        nc.sync.dma_start(w1_w[:].bitcast(I32), w1_words[0].bitcast(I32))
        nc.sync.dma_start(
            gain_sb[:].rearrange("p (b i) -> p b i", i=PACK), gain.rearrange("(b p i) -> p b i", p=P, i=PACK)
        )
        nc.sync.dma_start(atoms[:], offs2)

        tab_w = ring.tile([P, T], U32, name="tab_w", tag="slot_a", align_bytes=256)
        nc.sync.dma_start(tab_w[:].bitcast(I32), tab_words[0].rearrange("p t i -> p (t i)").bitcast(I32))
        for quad in range(4):
            nc.sync.dma_start(
                w1_s[32 * quad : 32 * quad + 4, :].bitcast(I32),
                w1_scales[0, 4 * quad : 4 * quad + 4, :].bitcast(I32),
            )

        nc.scalar.copy(
            w1p_w[:].bitcast(U16).rearrange("p (b i m) -> p b i m", b=PASSES, i=PACK),
            w1_w[:].rearrange("p (b m i) -> p b i m", b=PASSES, i=PACK),
        )
        nc.vector.tensor_copy(spread_s[:], tab_s[:].indirect(facts[:]))
        nc.gpsimd.tensor_copy(
            w1p_s[:].rearrange("p (b i m) -> p b i m", b=PASSES, i=PACK),
            w1_s[:].rearrange("p (b m i) -> p b i m", b=PASSES, i=PACK),
        )

        early = ring.tile([P, 2 * M], F32, name="early", tag="slot_w", align_bytes=256)
        wgt_sb = early[:, :M]
        c_view = c.rearrange("(b p i) m -> b p i m", p=P, i=PACK)
        w2_view = w2.rearrange("(b p i) n -> b p i n", p=P, i=PACK)

        nc.sync.dma_start(wgt_sb, wgt)
        nc.sync.dma_start(early[:, M:], c_view[0, :, 0, :])

        held = PLANES - 1
        late = ring.tile([P, held * M + PACK * N + N_TILES], F32, name="late", tag="slot_c", align_bytes=256)
        prior = [early[:, M:]] + [late[:, q * M : (q + 1) * M] for q in range(held)]
        prior1 = late[:, (held - PACK) * M : held * M].rearrange("p (i m) -> p i m", i=PACK)
        w2_last = ring.tile([P, PACK, N], F32, name="w2_last", tag="slot_s", align_bytes=256)
        w2_raw = [late[:, held * M : held * M + PACK * N].rearrange("p (i n) -> p i n", i=PACK), w2_last[:]]
        bias_sb = late[:, held * M + PACK * N :]
        for row in range(4):
            nc.sync.dma_start(v_s[row:P:32, :].bitcast(I32), spread_s[SPARE + row : P : 4, :].bitcast(I32))
        for q in range(1, PLANES):
            nc.sync.dma_start(prior[q], c_view[q // PACK, :, q % PACK, :])
        with nc.allow_non_contiguous_dma(reason="one bias value a partition"):
            nc.sync.dma_start(bias_sb, bias.rearrange("(t p) -> p t", p=P))
        for b in range(PASSES):
            nc.sync.dma_start(w2_raw[b], w2_view[b])

        wgt_ps = [psum.tile([P, BANK], F32, name="wgt_ps", tag="wgt_ps%d" % h) for h in range(M // BANK)]

        turns = []

        tag_of = {"wgt0": "wgt_ps0", "wgt1": "wgt_ps1"}

        def bank(name, after=None):
            if after is None:
                turns.append(name)
                tag_of[name] = "acc%d" % (len(turns) % ACC_BANKS)
            else:
                tag_of[name] = tag_of[after]
            return psum.tile([P, BANK], F32, name="bank", tag=tag_of[name])

        across = {}

        def wgt_forward(h):
            turned = psum.tile([P, BANK], F32, name="wgt_turned", tag="acc%d" % (h + 1))
            for k in range(PACK):
                m0 = h * BANK + k * P
                nc.tensor.transpose(turned[:, k * P : (k + 1) * P], wgt_sb[:, m0 : m0 + P], ident[:])
            across[h] = ring.tile([P, BANK], F32, name="across", tag="rounded%d0" % h, align_bytes=64)
            nc.scalar.activation(across[h][:], turned[:], ACT.Copy, scale=-1.0)

        def wgt_backward(h):
            for k in range(PACK):
                nc.tensor.transpose(wgt_ps[h][:, k * P : (k + 1) * P], across[h][:, k * P : (k + 1) * P], ident[:])

        zero = ring.tile([P, 1], F32, name="zero", tag="picked0", align_bytes=64)
        nc.gpsimd.memset(zero[:], 0.0)
        for q in range(PLANES - 1):
            nc.gpsimd.tensor_scalar(prior[q], prior[q], gain_sb[:, q : q + 1], zero[:], ALU.mult, ALU.add)
        for h, nothing in enumerate((zero[:], 0.0)):
            half = prior[PLANES - 1][:, h * BANK : (h + 1) * BANK]
            nc.gpsimd.tensor_scalar(half, half, gain_sb[:, PLANES - 1 :], nothing, ALU.mult, ALU.add)

        v_first = keep.tile([P, BANK], U32, name="v_first", align_bytes=64)
        v_rest = ring.tile([P, (SLICES - 1) * BANK], U32, name="v_rest", tag="slot_d", align_bytes=64)
        v_w = [v_first[:]] + [v_rest[:, s * BANK : (s + 1) * BANK] for s in range(SLICES - 1)]
        for s in range(SLICES):
            nc.vector.tensor_copy(v_w[s], tab_w[:].indirect(facts[:, s * BANK // 16 : (s + 1) * BANK // 16]))

        res = ring.tile([P, N_TILES, M], F32, name="res", tag="slot_a", align_bytes=256)

        truth = {}

        def first_product(q, s):
            if s == 0:
                truth[q] = ring.tile([P, S], F32, name="truth", tag="window%d" % (q % WINDOWS), align_bytes=64)
            acc = bank("acc%d%d" % (q, s))
            nc.tensor.matmul_mx(
                out=acc[:],
                lhsT=w1p_w[:, 2 * P * q : 2 * P * (q + 1)].bitcast(FP4X4),
                lhsT_scale=w1p_s[:, P * q : P * (q + 1)],
                rhs=v_w[s].bitcast(FP8X4),
                rhs_scale=v_s[:, s * BANK : (s + 1) * BANK],
                start=True,
                stop=True,
            )
            nc.scalar.activation(truth[q][:, s * BANK : (s + 1) * BANK], acc[:], ACT.Sigmoid)

        def truth_plane(q):
            for s in range(SLICES):
                first_product(q, s)

        slopes = {}


        def slope(q):
            slopes[q] = ring.tile([P, M], F32, name="slope", tag="slope%d" % q, align_bytes=64)
            for h in range(M // BANK):
                half = slice(h * BANK, (h + 1) * BANK)
                nc.vector.scalar_tensor_tensor(
                    slopes[q][:, half], prior[q][:, half], gain_sb[:, q : q + 1], wgt_ps[h][:], ALU.subtract, ALU.mult
                )

        picked0 = ring.tile([P, PACK, M], F32, name="picked0", tag="picked0", align_bytes=64)
        picked1 = {}

        def picked(q, m0, width):
            if q < PACK:
                return picked0[:, q, m0 : m0 + width]
            tile, first = picked1[m0 // CHUNK]
            return tile[:, q - PACK, m0 - first : m0 - first + width]

        def pick(q, m0=0, width=M):
            nc.vector.tensor_tensor(
                picked(q, m0, width),
                truth[q][:].indirect(atoms[:, m0 // 16 : (m0 + width) // 16]),
                slopes[q][:, m0 : m0 + width],
                ALU.mult,
            )

        def new_picked(j, chunks, tag):
            tile = ring.tile([P, PACK, CHUNK * chunks], F32, name="picked1", tag=tag, align_bytes=64)
            for k in range(chunks):
                picked1[j + k] = (tile, j * CHUNK)

        def pick_run(j, chunks, tag):
            new_picked(j, chunks, tag)
            for q in range(PACK, PLANES):
                pick(q, j * CHUNK, chunks * CHUNK)

        rounded = {}

        def new_rounded(g, j, chunks, tag):
            tile = ring.tile([P, 2 * CHUNK * chunks], BF16, name="rounded", tag=tag, align_bytes=64)
            for k in range(chunks):
                rounded[g, j + k] = (tile, j * CHUNK)

        turned = {}

        def turn(g, j, after=None):
            turned[g, j] = bank("turned%d%d" % (g, j), after)
            for k in range(CHUNK // P):
                m0 = j * CHUNK + k * P
                for e in range(2):
                    dst = turned[g, j][:, (2 * k + e) * P : (2 * k + e + 1) * P]
                    nc.tensor.matmul(
                        dst, prior[2 * g + e][:, m0 : m0 + P], ident[:], start=True, stop=False, is_transpose=True
                    )
                    nc.tensor.matmul(
                        dst, picked(2 * g + e, m0, P), ident[:], start=False, stop=True, is_transpose=True
                    )

        def round_pair(g, j):
            tile, first = rounded[g, j]
            m0 = j * CHUNK - first
            nc.scalar.copy(
                tile[:, 2 * m0 : 2 * (m0 + CHUNK)].rearrange("m (k p e) -> m k p e", k=2, e=2),
                turned[g, j][:].rearrange("m (k e p) -> m k p e", k=2, e=2),
            )

        def forward(g, j, after=None):
            turn(g, j, after)
            round_pair(g, j)

        zs = {}

        def new_z(b, j, chunks, tag):
            tile = ring.tile([P, PACK * CHUNK * chunks], BF16, name="z", tag=tag, align_bytes=64)
            for k in range(chunks):
                zs[b, j + k] = (tile, j * CHUNK)

        def z_cols(b, m0, width):
            tile, first = zs[b, m0 // CHUNK]
            return tile[:, PACK * (m0 - first) : PACK * (m0 - first + width)]

        def backward(b, j, after):
            back = bank("back%d%d" % (b, j), after)[:].rearrange("p (k u m) -> p k u m", u=2, m=P)
            for k in range(CHUNK // P):
                for u in range(2):
                    tile, first = rounded[2 * b + u, j]
                    m0 = j * CHUNK + k * P - first
                    nc.tensor.transpose(back[:, k, u, :], tile[:].bitcast(F32)[:, m0 : m0 + P], ident[:])
            nc.scalar.copy(
                z_cols(b, j * CHUNK, CHUNK).bitcast(F32).rearrange("p (k m u) -> p k m u", u=2, m=P),
                back.rearrange("p k u m -> p k m u"),
            )

        def join_on_vector(m0, width):
            tile, first = picked1[m0 // CHUNK]
            nc.vector.tensor_tensor(
                z_cols(1, m0, width).rearrange("p (c e i) -> p c i e", e=2, i=PACK),
                prior1[:, :, m0 : m0 + width].rearrange("p i (c e) -> p c i e", e=2),
                tile[:, :, m0 - first : m0 - first + width].rearrange("p i (c e) -> p c i e", e=2),
                ALU.add,
            )

        def quantise_z(b, m0, width):
            cols = slice(m0, m0 + width)
            nc.vector.quantize_mx(
                out=z_w[:, b, cols].bitcast(FP8X4),
                scales=z_s[:, b, cols],
                in_=z_cols(b, m0, width),
            )

        w2_bf = {}

        def round_w2(b, tag):
            w2_bf[b] = ring.tile([P, N * PACK], BF16, name="w2_bf", tag=tag, align_bytes=64)
            nc.scalar.copy(
                w2_bf[b][:].rearrange("p (c e i) -> p c i e", e=2, i=PACK),
                w2_raw[b].rearrange("p i (c e) -> p c i e", e=2),
            )

        def quantise_w2(b):
            nc.vector.quantize_mx(out=w2_w[:, b, :].bitcast(FP8X4), scales=w2_s[:, b, :], in_=w2_bf[b][:])

        out_view = out.rearrange("(t p) m -> p t m", p=P)

        evidence = {}

        def open_chunk(m0, after):
            for u in range(2):
                tile = bank("evidence%d_%d" % (m0, u), after[u])
                for half in range(2):
                    evidence[m0, 2 * u + half] = (tile[:, half * CHUNK : (half + 1) * CHUNK], half == 0, half == 1)

        def open_piece(m0, after):
            tiles = [bank("evidence%d_%d" % (m0, u), after[u]) for u in range(2)]
            for t in range(N_TILES):
                u, half = divmod(t, 2)
                evidence[m0, t] = (tiles[u][:, half * P : (half + 1) * P], half == 0, half == 1)

        def second_product(b, m0, width):
            cols = slice(m0, m0 + width)
            for t in range(N_TILES):
                acc, opens, closes = evidence[m0, t]
                nc.tensor.matmul_mx(
                    out=acc,
                    lhsT=w2_w[:, b, t * P : (t + 1) * P].bitcast(FP8X4),
                    lhsT_scale=w2_s[:, b, t * P : (t + 1) * P],
                    rhs=z_w[:, b, cols].bitcast(FP8X4),
                    rhs_scale=z_s[:, b, cols],
                    start=(b == 0 and opens),
                    stop=(b == PASSES - 1 and closes),
                )

        def store(m0, width, on_scalar):
            cols = slice(m0, m0 + width)
            for t in range(N_TILES):
                if t < on_scalar:
                    nc.scalar.activation(
                        res[:, t, cols], evidence[m0, t][0], ACT.Identity, bias=bias_sb[:, t : t + 1]
                    )
                else:
                    nc.vector.tensor_scalar(
                        res[:, t, cols], evidence[m0, t][0], bias_sb[:, t : t + 1], None, ALU.add
                    )
                if t % 2 == 1:
                    nc.sync.dma_start(out_view[:, t - 1 : t + 1, cols], res[:, t - 1 : t + 1, cols])

        wgt_forward(0)
        wgt_forward(1)
        first_product(0, 0)
        first_product(0, 1)
        for h in range(2):
            wgt_backward(h)
            first_product(1, h)
            first_product(0, 2 + h)
        for q in range(PLANES):
            slope(q)
        for s in range(2, SLICES):
            first_product(1, s)
        pick(0)
        truth_plane(2)
        pick(1)
        truth_plane(3)
        pick(2)
        round_w2(0, "w2_bf0")
        truth_plane(4)
        pick(3)
        truth_plane(5)
        for g in range(2):
            new_rounded(g, 0, 2, "rounded%d0" % g)
        turn(0, 2, "wgt0")
        turn(0, 3, "wgt1")
        for q in (6, 7):
            first_product(q, 0)
            first_product(q, 1)
            forward(0, q - 6)
            first_product(q, 2)
            first_product(q, 3)
        pick_run(0, 2, "picked1a")
        quantise_w2(0)

        new_z(0, 0, 2, "z_0")
        new_z(0, 2, 2, "z_1")
        new_z(1, 0, 1, "z_a")
        new_z(1, 1, 1, "z_b")
        forward(1, 0)
        forward(1, 1)
        for g in range(2):
            new_rounded(g, 2, 2, "rounded%d1" % g)
            new_rounded(2 + g, 0, 1, "slope%d" % g)
        round_pair(0, 2)
        round_pair(0, 3)
        backward(0, 0, "acc72")
        backward(0, 1, "acc73")
        round_w2(1, "rounded00")
        join_on_vector(CHUNK, CHUNK)
        pick_run(2, 1, "picked1b")
        new_z(1, 2, 1, "slope2")
        join_on_vector(2 * CHUNK, CHUNK)
        forward(1, 2, "turned10")
        forward(1, 3, "turned11")
        forward(2, 0, "turned02")
        forward(3, 0, "turned03")
        backward(0, 2, "acc71")
        backward(0, 3, "turned01")
        backward(1, 0, "back00")
        quantise_z(0, 0, 2 * CHUNK)
        quantise_w2(1)
        quantise_z(1, CHUNK, CHUNK)
        open_chunk(CHUNK, ("back01", "turned12"))
        second_product(0, CHUNK, CHUNK)
        second_product(1, CHUNK, CHUNK)
        quantise_z(1, 2 * CHUNK, CHUNK)
        quantise_z(0, 2 * CHUNK, 2 * CHUNK)
        open_chunk(2 * CHUNK, ("turned13", "turned20"))
        second_product(0, 2 * CHUNK, CHUNK)
        second_product(1, 2 * CHUNK, CHUNK)
        store(CHUNK, CHUNK, N_TILES)
        open_chunk(0, ("turned30", "back02"))
        second_product(0, 0, CHUNK)
        open_piece(3 * CHUNK, ("back03", "back10"))
        second_product(0, 3 * CHUNK, P)
        open_piece(3 * CHUNK + P, ("evidence%d_0" % CHUNK, "evidence%d_1" % CHUNK))
        second_product(0, 3 * CHUNK + P, P)
        quantise_z(1, 0, CHUNK)
        second_product(1, 0, CHUNK)
        store(2 * CHUNK, CHUNK, N_TILES)
        pick_run(3, 1, "slope0")
        new_z(1, 3, 1, "z_b")
        for h in range(2):
            join_on_vector(3 * CHUNK + h * P, P)
        store(0, CHUNK, N_TILES)
        for h in range(2):
            quantise_z(1, 3 * CHUNK + h * P, P)
            second_product(1, 3 * CHUNK + h * P, P)
        for h in range(2):
            store(3 * CHUNK + h * P, P, N_TILES // 2)
